import numpy as np
import ml_dtypes


def mxq(x, axis, fmt="e4m3"):
    dtype, down = {"e4m3": (ml_dtypes.float8_e4m3fn, 7), "e5m2": (ml_dtypes.float8_e5m2, 14)}[fmt]
    v = np.moveaxis(np.asarray(x, np.float32).astype(ml_dtypes.bfloat16).astype(np.float64), axis, -1)
    blocks = v.reshape(v.shape[:-1] + (-1, 32))
    amax = np.abs(blocks).max(-1, keepdims=True)
    byte = np.maximum(np.where(amax > 0, np.frexp(amax)[1] - 1 + 127, 0) - down, 1)
    scale = np.exp2(byte - 127.0)
    codes = (blocks / scale).astype(np.float32).astype(dtype).astype(np.float64)
    return np.moveaxis((codes * scale).reshape(v.shape), -1, axis)


WIDE = False


def mx_kscale(k):
    if not WIDE:
        return np.ones(k)
    levels = np.array([10, -10, 5, -5, 0])
    if k % 512:
        return np.exp2(np.random.permutation(np.resize(levels, k // 32))).repeat(32)
    a = np.empty((k // 512, 16))
    for p in range(k // 512):
        a[p, :8] = np.random.permutation(np.resize(levels, 8))
        for g in range(8):
            far = levels[np.abs(levels - a[p, g]) >= 10]
            a[p, g + 8] = far[np.random.randint(len(far))]
    return np.exp2(a.ravel()).repeat(32)


BF16 = ml_dtypes.bfloat16


def bf(x):
    return np.asarray(x, np.float32).astype(BF16)


def f64(x):
    return np.asarray(x).astype(np.float64)


E2M1 = np.array([0.0, 0.5, 1.0, 1.5, 2.0, 3.0, 4.0, 6.0, -0.0, -0.5, -1.0, -1.5, -2.0, -3.0, -4.0, -6.0])


def pack_weight(w, fmt):
    k, n = w.shape
    w = f64(bf(w)).reshape(k // 32, 32, n)
    amax = np.abs(w).max(1)
    if fmt == "e4m3":
        byte = np.frexp(amax)[1] - 1 + 127 - 7
    else:
        mant, ex = np.frexp(amax / 6.0)
        byte = np.where(mant > 0.5, ex, ex - 1) + 127
    byte = np.clip(np.where(amax > 0, byte, 1), 1, 254)
    scaled = (w * np.exp2(127.0 - byte)[:, None, :]).reshape(k, n).astype(np.float32)
    by_word = np.ascontiguousarray(scaled.reshape(k // 512, 128, 4, n).transpose(0, 1, 3, 2))
    if fmt == "e4m3":
        words = by_word.astype(ml_dtypes.float8_e4m3fn).view(np.uint8)
    else:
        c = by_word.astype(ml_dtypes.float4_e2m1fn).view(np.uint8) & 0xF
        words = c[..., 0::2] | (c[..., 1::2] << 4)
    return np.ascontiguousarray(words), np.ascontiguousarray(byte.astype(np.uint8).reshape(k // 512, 16, n))


def unpack_weight(words, scales, fmt):
    g, p, n, _ = words.shape
    if fmt == "e4m3":
        vals = np.ascontiguousarray(words).view(ml_dtypes.float8_e4m3fn).astype(np.float64)
    else:
        nib = np.empty((g, p, n, 4), np.uint8)
        nib[..., 0::2] = words & 0xF
        nib[..., 1::2] = words >> 4
        vals = E2M1[nib]
    vals = vals * np.repeat(np.exp2(scales.astype(np.float64) - 127.0), 8, axis=1)[..., None]
    return vals.transpose(0, 1, 3, 2).reshape(g * 512, n)
def pack4(w):
    words, scales = pack_weight(w, "e2m1")
    return words.reshape(words.shape[0], 128, -1), scales


def unpack4(words, scales):
    return unpack_weight(words.reshape(words.shape[0], 128, -1, 2), scales, "e2m1")


def planes(Y):
    n, m = Y.shape
    b = f64(bf(Y)).reshape(n // 32, 32, m)
    amax = np.abs(b).max(1)
    byte = np.clip(np.where(amax > 0, np.frexp(amax)[1] - 1 + 127 - 7, 1), 1, 254)
    codes = (b * np.exp2(127.0 - byte)[:, None, :]).reshape(n, m).astype(np.float32).astype(ml_dtypes.float8_e4m3fn).view(np.uint8)
    words = codes.reshape(n // 512, 128, 4, m).transpose(0, 1, 3, 2)
    return np.ascontiguousarray(words), np.ascontiguousarray(byte.astype(np.uint8).reshape(n // 512, 16, m))


R, D, C = 2048, 1536, 512


def setup_inputs():
    s = mx_kscale(D)
    t = mx_kscale(R)
    X = np.random.randn(R, D)
    a_words, a_scales = pack4(X.T * s[:, None])
    f_words, f_scales = pack4(X / np.sqrt(R) * t[:, None])
    return {
        "a_words": a_words,
        "a_scales": a_scales,
        "f_words": f_words,
        "f_scales": f_scales,
        "coef": bf(2.0 * np.random.randn(D, C) / np.sqrt(D) / s[:, None]),
        "labels": bf(np.random.rand(R, C) < 0.5),
        "row_weight": bf(np.exp(0.3 * np.random.randn(R)) / t),
        "carry": bf(0.5 * np.random.randn(D, C)),
        "diag": bf(1.5 * np.exp(0.8 * np.random.randn(D))),
    }


def reference(a_words, a_scales, f_words, f_scales, coef, labels, row_weight, carry, diag):
    A = unpack4(a_words, a_scales)
    F = unpack4(f_words, f_scales)
    Z = A.T @ mxq(f64(coef), 0, "e4m3")
    E = f64(row_weight)[:, None] * (1.0 / (1.0 + np.exp(-Z)) - f64(labels))
    G = F.T @ mxq(E, 0, "e4m3")
    y = f64(diag)[:, None] * (G + f64(carry))
    Y = y.reshape(D, C)
    words, scales = planes(Y)
    return y, words, scales

@@ -1,0 +1,371 @@
+from contextlib import ExitStack
+
+import concourse.mybir as mybir
+from concourse.masks import make_identity
+
+R, D, C = 2048, 1536, 512
+FLOPS = 2 * 2 * R * D * C
+
+F32 = mybir.dt.float32
+BF16 = mybir.dt.bfloat16
+I32 = mybir.dt.int32
+U32 = mybir.dt.uint32
+U8 = mybir.dt.uint8
+FP8X4 = mybir.dt.float8_e4m3fn_x4
+FP4X4 = mybir.dt.float4_e2m1fn_x4
+ALU = mybir.AluOpType
+ACT = mybir.ActivationFunctionType
+
+P = 128
+PACK = 4
+GROUP = P * PACK
+DG = D // GROUP
+RG = R // GROUP
+HALF = C // 2
+
+
+def tile_preconditioned_logistic_gradient_h1_kernel(
+    tc, a_words, a_scales, f_words, f_scales, coef, labels, row_weight, carry, diag, out_0, out_1, out_2
+):
+    nc = tc.nc
+    with ExitStack() as ctx:
+        keep = ctx.enter_context(tc.tile_pool(name="keep", bufs=1))
+        work = ctx.enter_context(tc.tile_pool(name="work", bufs=1))
+        psum = ctx.enter_context(tc.psum_pool(name="psum", bufs=1))
+        ctx.enter_context(tc.manual_schedule())
+
+        def kept(name, shape, dtype):
+            return keep.tile(shape, dtype, name=name, align_bytes=64)
+
+        def bank(b):
+            return psum.tile([P, GROUP], F32, name="bank%d" % b)
+
+        def interleave(engine_copy, dst, src):
+            engine_copy(
+                out=dst.rearrange("p (c i) t -> p c t i", i=4),
+                in_=src.rearrange("p t (c i) -> p c t i", i=4),
+            )
+
+        def quantize(codes, scales, src):
+            nc.vector.quantize_mx(out=codes.bitcast(FP8X4), scales=scales, in_=src.rearrange("p c t -> p (c t)"))
+
+        a_sb = [kept("a_sb%d" % rp, [P, DG, 2 * 2 * GROUP], U8) for rp in range(2)]
+        a_sc = [kept("a_sc%d" % rp, [P, DG, 2 * GROUP], U8) for rp in range(2)]
+        f_sb = [kept("f_sb%d" % dg, [P, RG, 2 * GROUP], U8) for dg in range(DG)]
+        f_sc = kept("f_sc", [P, RG, D], U8)
+        coef_sb = [kept("coef_sb%d" % dg, [P, PACK, C], BF16) for dg in range(DG)]
+        coef_il = [kept("coef_il%d" % dg, [P, C, PACK], BF16) for dg in range(DG)]
+        coef_q = [kept("coef_q%d" % dg, [P, C], U32) for dg in range(DG)]
+        coef_s = [kept("coef_s%d" % dg, [P, C], U8) for dg in range(DG)]
+        lab_sb = [kept("lab_sb%d" % g, [P, PACK, C], BF16) for g in range(RG)]
+        lw_sb = [kept("lw_sb%d" % g, [P, PACK, C], BF16) for g in range(RG)]
+        e_q = [kept("e_q%d" % g, [P, C], U32) for g in range(RG)]
+        e_s = [kept("e_s%d" % g, [P, C], U8) for g in range(RG)]
+        carry_sb = [kept("carry_sb%d" % dg, [P, PACK, C], BF16) for dg in range(DG)]
+        y_sb = [kept("y_sb%d" % dg, [P, PACK, C], F32) for dg in range(DG)]
+        y_q = [kept("y_q%d" % dg, [P, C], U32) for dg in range(DG)]
+        y_s = kept("y_s", [P, DG, C], U8)
+        w_bf = kept("w_bf", [P, RG, PACK], BF16)
+        w_f32 = kept("w_f32", [P, RG, PACK], F32)
+        d_bf = kept("d_bf", [P, DG, PACK], BF16)
+        d_f32 = kept("d_f32", [P, DG, PACK], F32)
+        ident = kept("ident", [P, P], F32)
+        warm = kept("warm", [P, 1], F32)
+
+        def load_scale_rows(plane, rows):
+            by_r = rows.rearrange("g (q r) n -> r q g n", r=4)
+            for r in range(4):
+                nc.sync.dma_start(out=plane[r:P:32, :, :].bitcast(I32), in_=by_r[r].bitcast(I32))
+
+        def load_rows(dst, src, g):
+            nc.sync.dma_start(out=dst[:], in_=src[g * GROUP : (g + 1) * GROUP, :].rearrange("(p t) c -> p t c", t=PACK))
+
+        a_by_p = a_words.rearrange("g p n -> p g n")
+        f_by_p = f_words.rearrange("g p n -> p g n")
+
+        for rp in range(2):
+            nc.vector.memset(a_sc[rp][:].bitcast(I32), 0)
+        nc.vector.memset(warm[:], 0.0)
+        make_identity(nc, ident[:])
+        nc.gpsimd.memset(f_sc[:].bitcast(I32), 0)
+        nc.scalar.dma_start(out=w_bf[:], in_=row_weight.rearrange("(g p t) -> p g t", p=P, t=PACK))
+        nc.scalar.dma_start(out=d_bf[:], in_=diag.rearrange("(g p t) -> p g t", p=P, t=PACK))
+        nc.scalar.activation(out=warm[:], in_=warm[:], func=ACT.Sigmoid)
+        nc.gpsimd.tensor_copy(out=w_f32[:], in_=w_bf[:])
+        nc.gpsimd.tensor_copy(out=d_f32[:], in_=d_bf[:])
+
+        for dg in range(DG):
+            load_rows(coef_sb[dg], coef, dg)
+            if dg == 0:
+                load_scale_rows(a_sc[0], a_scales[:, :, 0 : 2 * GROUP])
+            nc.sync.dma_start(out=a_sb[0][:, dg, :].bitcast(I32), in_=a_by_p[:, dg, 0 : 4 * GROUP].bitcast(I32))
+        load_scale_rows(a_sc[1], a_scales[:, :, 2 * GROUP :])
+        nc.sync.dma_start(out=a_sb[1][:].bitcast(I32), in_=a_by_p[:, :, 4 * GROUP :].bitcast(I32))
+        for g in range(RG):
+            load_rows(lab_sb[g], labels, g)
+        load_scale_rows(f_sc, f_scales)
+        for dg in range(DG):
+            nc.sync.dma_start(
+                out=f_sb[dg][:].bitcast(I32), in_=f_by_p[:, :, 2 * GROUP * dg : 2 * GROUP * (dg + 1)].bitcast(I32)
+            )
+        for dg in range(DG):
+            load_rows(carry_sb[dg], carry, dg)
+
+        for dg in range(DG):
+            tiles = [slice(i * P, (i + 1) * P) for i in range(2)]
+            for cols in tiles:
+                interleave(nc.vector.tensor_copy, coef_il[dg][:, cols, :], coef_sb[dg][:, :, cols])
+            interleave(nc.scalar.copy, coef_il[dg][:, HALF:, :], coef_sb[dg][:, :, HALF:])
+            for cols in tiles:
+                quantize(coef_q[dg][:, cols], coef_s[dg][:, cols], coef_il[dg][:, cols, :])
+        for dg in range(DG):
+            quantize(coef_q[dg][:, HALF:], coef_s[dg][:, HALF:], coef_il[dg][:, HALF:, :])
+
+        def label_weights(g):
+            for t in range(PACK):
+                nc.vector.tensor_scalar(
+                    out=lw_sb[g][:, t, :], in0=lab_sb[g][:, t, :], scalar1=w_f32[:, g, t : t + 1], scalar2=None, op0=ALU.mult
+                )
+
+        def carry_diag(dg):
+            for t in range(PACK):
+                nc.scalar.activation(
+                    out=y_sb[dg][:, t, :], in_=carry_sb[dg][:, t, :], func=ACT.Copy, scale=d_f32[:, dg, t : t + 1]
+                )
+
+        def c_tile(h, i):
+            return slice(HALF * h + P * i, HALF * h + P * (i + 1))
+
+        def half(h):
+            return slice(HALF * h, HALF * (h + 1))
+
+        sums = {}
+        turned_src = {}
+        turned = {}
+        flat = {}
+        grouped = {}
+
+        def logit_pass(h, g, i, dg):
+            rp, lo = divmod(g, 2)
+            nc.tensor.matmul_mx(
+                out=sums[("e", h, g, i)][:],
+                lhsT=coef_q[dg][:, c_tile(h, i)].bitcast(FP8X4),
+                lhsT_scale=coef_s[dg][:, c_tile(h, i)],
+                rhs=a_sb[rp][:, dg, 2 * GROUP * lo : 2 * GROUP * (lo + 1)].bitcast(FP4X4),
+                rhs_scale=a_sc[rp][:, dg, GROUP * lo : GROUP * (lo + 1)],
+                start=(dg == 0),
+                stop=(dg == DG - 1),
+            )
+
+        def grad_pass(h, dg, i, g):
+            nc.tensor.matmul_mx(
+                out=sums[("y", h, dg, i)][:],
+                lhsT=e_q[g][:, c_tile(h, i)].bitcast(FP8X4),
+                lhsT_scale=e_s[g][:, c_tile(h, i)],
+                rhs=f_sb[dg][:, g, :].bitcast(FP4X4),
+                rhs_scale=f_sc[:, g, GROUP * dg : GROUP * (dg + 1)],
+                start=(g == 0),
+                stop=(g == RG - 1),
+            )
+
+        def multiply(kind, h, g, banks, pass_major=False):
+            one, n = (logit_pass, DG) if kind == "e" else (grad_pass, RG)
+            keys = [(gg, i) for gg in g for i in range(2)]
+            for (gg, i), b in zip(keys, banks):
+                sums[(kind, h, gg, i)] = bank(b)
+            if pass_major:
+                for k in range(n):
+                    for gg, i in keys:
+                        one(h, gg, i, k)
+            else:
+                for gg, i in keys:
+                    for k in range(n):
+                        one(h, gg, i, k)
+
+        def empty(kind, h, g, i):
+            src = sums[(kind, h, g, i)][:].rearrange("c (p t) -> c t p", t=PACK)
+            dst = work.tile([P, PACK, P], F32, name="turn_src", bufs=8)
+            turned_src[(kind, h, g, i)] = dst
+            if kind == "e":
+                nc.scalar.activation(out=dst[:], in_=src, func=ACT.Sigmoid)
+            else:
+                nc.scalar.copy(out=dst[:], in_=src)
+
+        def turn(kind, h, g, banks):
+            pair = [bank(b) for b in banks]
+            turned[(kind, h, g)] = pair
+            for i in range(2):
+                for t in range(PACK):
+                    lo = HALF * (t % 2) + P * i
+                    nc.tensor.transpose(pair[t // 2][:, lo : lo + P], turned_src[(kind, h, g, i)][:, t, :], ident[:])
+
+        def combine(kind, h, g):
+            pair = turned[(kind, h, g)]
+            if kind == "e":
+                dst = work.tile([P, PACK, HALF], BF16, name="e_flat", bufs=3)
+                flat[(kind, h, g)] = dst[:]
+            else:
+                flat[(kind, h, g)] = y_sb[g][:, :, half(h)]
+            for t in range(PACK):
+                src = pair[t // 2][:, HALF * (t % 2) : HALF * (t % 2 + 1)]
+                if kind == "e":
+                    nc.vector.scalar_tensor_tensor(
+                        out=dst[:, t, :], in0=src, scalar=w_f32[:, g, t : t + 1], in1=lw_sb[g][:, t, half(h)],
+                        op0=ALU.mult, op1=ALU.subtract,
+                    )
+                else:
+                    nc.vector.scalar_tensor_tensor(
+                        out=y_sb[g][:, t, half(h)], in0=src, scalar=d_f32[:, g, t : t + 1], in1=y_sb[g][:, t, half(h)],
+                        op0=ALU.mult, op1=ALU.add,
+                    )
+            if kind == "y":
+                nc.sync.dma_start(
+                    out=out_0[g * GROUP : (g + 1) * GROUP, half(h)].rearrange("(p t) c -> p t c", t=PACK),
+                    in_=y_sb[g][:, :, half(h)],
+                )
+
+        def group(kind, h, g, engine_copy):
+            dst = work.tile([P, HALF, PACK], BF16, name="grouped", bufs=3, align_bytes=64)
+            grouped[(kind, h, g)] = dst
+            interleave(engine_copy, dst[:], flat[(kind, h, g)])
+
+        def finish(kind, h, g):
+            if kind == "e":
+                quantize(e_q[g][:, half(h)], e_s[g][:, half(h)], grouped[(kind, h, g)][:])
+            else:
+                quantize(y_q[g][:, half(h)], y_s[:, g, half(h)], grouped[(kind, h, g)][:])
+                nc.sync.dma_start(
+                    out=out_1[g].rearrange("p c t -> p (c t)")[:, PACK * HALF * h : PACK * HALF * (h + 1)].bitcast(I32),
+                    in_=y_q[g][:, half(h)].bitcast(I32),
+                )
+
+        LO, HI = [0, 1, 2, 3], [4, 5, 6, 7]
+        V, S = nc.vector.tensor_copy, nc.scalar.copy
+
+        multiply("e", 0, [0, 1], LO, pass_major=True)
+        label_weights(0)
+        label_weights(1)
+        for g in (0, 1):
+            for i in range(2):
+                empty("e", 0, g, i)
+        multiply("e", 0, [2, 3], HI)
+        for g in (2, 3):
+            for i in range(2):
+                empty("e", 0, g, i)
+
+        rounds = [
+            ([("e", 0, 0), ("e", 0, 1)], [("e", 1, 0), ("e", 1, 1)]),
+            ([("e", 0, 2), ("e", 0, 3)], [("e", 1, 2), ("e", 1, 3)]),
+            ([("e", 1, 0), ("e", 1, 1)], [("y", 0, 0), ("y", 0, 1)]),
+        ]
+        for n, (old, new) in enumerate(rounds):
+            turn(*old[0], LO[:2])
+            turn(*old[1], LO[2:])
+            multiply(new[0][0], new[0][1], [new[0][2], new[1][2]], HI)
+            combine(*old[0])
+            combine(*old[1])
+            empty(*new[0], 0)
+            group(*old[0], S)
+            empty(*new[0], 1)
+            empty(*new[1], 0)
+            empty(*new[1], 1)
+            if n == 0:
+                label_weights(2)
+                label_weights(3)
+            group(*old[1], V)
+            finish(*old[0])
+            finish(*old[1])
+        carry_diag(0)
+
+        turn("e", 1, 2, LO[:2])
+        turn("e", 1, 3, LO[2:])
+        multiply("y", 0, [2], HI[:2])
+        combine("e", 1, 2)
+        combine("e", 1, 3)
+        group("e", 1, 2, S)
+        empty("y", 0, 2, 0)
+        empty("y", 0, 2, 1)
+        carry_diag(1)
+        group("e", 1, 3, V)
+        finish("e", 1, 2)
+        finish("e", 1, 3)
+
+        turn("y", 0, 0, LO[:2])
+        turn("y", 0, 1, LO[2:])
+        multiply("y", 1, [0], HI[2:], pass_major=True)
+        multiply("y", 1, [1], HI[:2])
+        combine("y", 0, 0)
+        combine("y", 0, 1)
+        empty("y", 1, 0, 0)
+        empty("y", 1, 0, 1)
+        carry_diag(2)
+        empty("y", 1, 1, 0)
+        empty("y", 1, 1, 1)
+        group("y", 0, 0, V)
+        group("y", 0, 1, V)
+        finish("y", 0, 0)
+        finish("y", 0, 1)
+
+        def last_multiply(i):
+            sums[("y", 1, 2, i)] = bank(HI[2 + i])
+            for k in range(RG):
+                grad_pass(1, 2, i, k)
+
+        def last_turn(i):
+            dst = bank(LO[2 + i])
+            turned[("last", i)] = dst
+            for t in range(PACK):
+                nc.tensor.transpose(dst[:, P * t : P * (t + 1)], turned_src[("y", 1, 2, i)][:, t, :], ident[:])
+
+        def last_combine(i):
+            cols = c_tile(1, i)
+            for t in range(PACK):
+                nc.vector.scalar_tensor_tensor(
+                    out=y_sb[2][:, t, cols], in0=turned[("last", i)][:, P * t : P * (t + 1)], scalar=d_f32[:, 2, t : t + 1],
+                    in1=y_sb[2][:, t, cols], op0=ALU.mult, op1=ALU.add,
+                )
+            nc.sync.dma_start(
+                out=out_0[2 * GROUP :, cols].rearrange("(p t) c -> p t c", t=PACK), in_=y_sb[2][:, :, cols]
+            )
+
+        def last_group(i, engine_copy):
+            dst = work.tile([P, P, PACK], BF16, name="last_grouped", bufs=2, align_bytes=64)
+            grouped[("last", i)] = dst
+            interleave(engine_copy, dst[:], y_sb[2][:, :, c_tile(1, i)])
+
+        def last_finish(i):
+            cols = c_tile(1, i)
+            quantize(y_q[2][:, cols], y_s[:, 2, cols], grouped[("last", i)][:])
+
+        turn("y", 0, 2, LO[:2])
+        turn("y", 1, 0, LO[2:])
+        last_multiply(0)
+        combine("y", 0, 2)
+        combine("y", 1, 0)
+        group("y", 0, 2, S)
+        empty("y", 1, 2, 0)
+        turn("y", 1, 1, LO[:2])
+        last_multiply(1)
+        empty("y", 1, 2, 1)
+        last_turn(0)
+        last_turn(1)
+        group("y", 1, 0, S)
+        combine("y", 1, 1)
+        finish("y", 0, 2)
+        group("y", 1, 1, S)
+        last_combine(0)
+        finish("y", 1, 0)
+        last_combine(1)
+        last_group(0, V)
+        last_group(1, V)
+        finish("y", 1, 1)
+        last_finish(0)
+        last_finish(1)
+        nc.scalar.dma_start(
+            out=out_1[2].rearrange("p c t -> p (c t)")[:, PACK * HALF :].bitcast(I32), in_=y_q[2][:, HALF:].bitcast(I32)
+        )
+
+        by_r = out_2.rearrange("g (q r) c -> r q g c", r=4)
+        for r in range(4):
+            queue = nc.scalar if r % 2 else nc.sync
+            queue.dma_start(out=by_r[r].bitcast(I32), in_=y_s[r:P:32, :, :].bitcast(I32))

@@ -17,11 +17,19 @@ ALU = mybir.AluOpType
 ACT = mybir.ActivationFunctionType
 
 P = 128
-PACK = 4
-GROUP = P * PACK
-DG = D // GROUP
-RG = R // GROUP
+SLOTS = 4
+GROUP = P * SLOTS
+FEATURE_GROUPS = D // GROUP
+ROW_GROUPS = R // GROUP
 HALF = C // 2
+WORD4 = 2
+QUADRANT = 32
+SCALE_RUN = 4
+BANKS = 8
+EARLY_ROWS = 2 * GROUP
+DIRECT = 2
+LAST = FEATURE_GROUPS - 1
+ERR, OUT = "errors", "outputs"
 
 
 def tile_preconditioned_logistic_gradient_h1_kernel(
@@ -33,339 +41,466 @@ def tile_preconditioned_logistic_gradient_h1_kernel(
         work = ctx.enter_context(tc.tile_pool(name="work", bufs=1))
         psum = ctx.enter_context(tc.psum_pool(name="psum", bufs=1))
         ctx.enter_context(tc.manual_schedule())
+        on_vector, on_scalar = nc.vector.tensor_copy, nc.scalar.copy
 
         def kept(name, shape, dtype):
             return keep.tile(shape, dtype, name=name, align_bytes=64)
 
-        def bank(b):
-            return psum.tile([P, GROUP], F32, name="bank%d" % b)
+        free_banks = list(range(BANKS))
+        bank_of = {}
 
-        def interleave(engine_copy, dst, src):
-            engine_copy(
-                out=dst.rearrange("p (c i) t -> p c t i", i=4),
-                in_=src.rearrange("p t (c i) -> p c t i", i=4),
-            )
+        def take_bank(key):
+            bank_of[key] = free_banks.pop(0)
+            return psum.tile([P, GROUP], F32, name="bank%d" % bank_of[key])
 
-        def quantize(codes, scales, src):
-            nc.vector.quantize_mx(out=codes.bitcast(FP8X4), scales=scales, in_=src.rearrange("p c t -> p (c t)"))
-
-        a_sb = [kept("a_sb%d" % rp, [P, DG, 2 * 2 * GROUP], U8) for rp in range(2)]
-        a_sc = [kept("a_sc%d" % rp, [P, DG, 2 * GROUP], U8) for rp in range(2)]
-        f_sb = [kept("f_sb%d" % dg, [P, RG, 2 * GROUP], U8) for dg in range(DG)]
-        f_sc = kept("f_sc", [P, RG, D], U8)
-        coef_sb = [kept("coef_sb%d" % dg, [P, PACK, C], BF16) for dg in range(DG)]
-        coef_il = [kept("coef_il%d" % dg, [P, C, PACK], BF16) for dg in range(DG)]
-        coef_q = [kept("coef_q%d" % dg, [P, C], U32) for dg in range(DG)]
-        coef_s = [kept("coef_s%d" % dg, [P, C], U8) for dg in range(DG)]
-        lab_sb = [kept("lab_sb%d" % g, [P, PACK, C], BF16) for g in range(RG)]
-        lw_sb = [kept("lw_sb%d" % g, [P, PACK, C], BF16) for g in range(RG)]
-        e_q = [kept("e_q%d" % g, [P, C], U32) for g in range(RG)]
-        e_s = [kept("e_s%d" % g, [P, C], U8) for g in range(RG)]
-        carry_sb = [kept("carry_sb%d" % dg, [P, PACK, C], BF16) for dg in range(DG)]
-        y_sb = [kept("y_sb%d" % dg, [P, PACK, C], F32) for dg in range(DG)]
-        y_q = [kept("y_q%d" % dg, [P, C], U32) for dg in range(DG)]
-        y_s = kept("y_s", [P, DG, C], U8)
-        w_bf = kept("w_bf", [P, RG, PACK], BF16)
-        w_f32 = kept("w_f32", [P, RG, PACK], F32)
-        d_bf = kept("d_bf", [P, DG, PACK], BF16)
-        d_f32 = kept("d_f32", [P, DG, PACK], F32)
-        ident = kept("ident", [P, P], F32)
-        warm = kept("warm", [P, 1], F32)
-
-        def load_scale_rows(plane, rows):
-            by_r = rows.rearrange("g (q r) n -> r q g n", r=4)
-            for r in range(4):
-                nc.sync.dma_start(out=plane[r:P:32, :, :].bitcast(I32), in_=by_r[r].bitcast(I32))
-
-        def load_rows(dst, src, g):
-            nc.sync.dma_start(out=dst[:], in_=src[g * GROUP : (g + 1) * GROUP, :].rearrange("(p t) c -> p t c", t=PACK))
-
-        a_by_p = a_words.rearrange("g p n -> p g n")
-        f_by_p = f_words.rearrange("g p n -> p g n")
-
-        for rp in range(2):
-            nc.vector.memset(a_sc[rp][:].bitcast(I32), 0)
-        nc.vector.memset(warm[:], 0.0)
-        make_identity(nc, ident[:])
-        nc.gpsimd.memset(f_sc[:].bitcast(I32), 0)
-        nc.scalar.dma_start(out=w_bf[:], in_=row_weight.rearrange("(g p t) -> p g t", p=P, t=PACK))
-        nc.scalar.dma_start(out=d_bf[:], in_=diag.rearrange("(g p t) -> p g t", p=P, t=PACK))
-        nc.scalar.activation(out=warm[:], in_=warm[:], func=ACT.Sigmoid)
-        nc.gpsimd.tensor_copy(out=w_f32[:], in_=w_bf[:])
-        nc.gpsimd.tensor_copy(out=d_f32[:], in_=d_bf[:])
-
-        for dg in range(DG):
-            load_rows(coef_sb[dg], coef, dg)
-            if dg == 0:
-                load_scale_rows(a_sc[0], a_scales[:, :, 0 : 2 * GROUP])
-            nc.sync.dma_start(out=a_sb[0][:, dg, :].bitcast(I32), in_=a_by_p[:, dg, 0 : 4 * GROUP].bitcast(I32))
-        load_scale_rows(a_sc[1], a_scales[:, :, 2 * GROUP :])
-        nc.sync.dma_start(out=a_sb[1][:].bitcast(I32), in_=a_by_p[:, :, 4 * GROUP :].bitcast(I32))
-        for g in range(RG):
-            load_rows(lab_sb[g], labels, g)
-        load_scale_rows(f_sc, f_scales)
-        for dg in range(DG):
-            nc.sync.dma_start(
-                out=f_sb[dg][:].bitcast(I32), in_=f_by_p[:, :, 2 * GROUP * dg : 2 * GROUP * (dg + 1)].bitcast(I32)
-            )
-        for dg in range(DG):
-            load_rows(carry_sb[dg], carry, dg)
-
-        for dg in range(DG):
-            tiles = [slice(i * P, (i + 1) * P) for i in range(2)]
-            for cols in tiles:
-                interleave(nc.vector.tensor_copy, coef_il[dg][:, cols, :], coef_sb[dg][:, :, cols])
-            interleave(nc.scalar.copy, coef_il[dg][:, HALF:, :], coef_sb[dg][:, :, HALF:])
-            for cols in tiles:
-                quantize(coef_q[dg][:, cols], coef_s[dg][:, cols], coef_il[dg][:, cols, :])
-        for dg in range(DG):
-            quantize(coef_q[dg][:, HALF:], coef_s[dg][:, HALF:], coef_il[dg][:, HALF:, :])
-
-        def label_weights(g):
-            for t in range(PACK):
-                nc.vector.tensor_scalar(
-                    out=lw_sb[g][:, t, :], in0=lab_sb[g][:, t, :], scalar1=w_f32[:, g, t : t + 1], scalar2=None, op0=ALU.mult
-                )
-
-        def carry_diag(dg):
-            for t in range(PACK):
-                nc.scalar.activation(
-                    out=y_sb[dg][:, t, :], in_=carry_sb[dg][:, t, :], func=ACT.Copy, scale=d_f32[:, dg, t : t + 1]
-                )
-
-        def c_tile(h, i):
-            return slice(HALF * h + P * i, HALF * h + P * (i + 1))
+        def give_bank(key):
+            free_banks.append(bank_of[key])
 
         def half(h):
             return slice(HALF * h, HALF * (h + 1))
 
+        def targets(h, i):
+            return slice(HALF * h + P * i, HALF * h + P * (i + 1))
+
+        a_sb = [kept("a_sb%d" % n, [P, FEATURE_GROUPS, WORD4 * EARLY_ROWS], U8) for n in range(2)]
+        a_sc = [kept("a_sc%d" % n, [P, FEATURE_GROUPS, EARLY_ROWS], U8) for n in range(2)]
+        f_sb = [kept("f_sb%d" % n, [P, ROW_GROUPS, WORD4 * GROUP], U8) for n in range(FEATURE_GROUPS)]
+        f_sc = kept("f_sc", [P, ROW_GROUPS, D], U8)
+        coef_sb = [kept("coef_sb%d" % n, [P, SLOTS, C], BF16) for n in range(FEATURE_GROUPS)]
+        coef_packed = [kept("coef_packed%d" % n, [P, C, SLOTS], BF16) for n in range(FEATURE_GROUPS)]
+        coef_q = [kept("coef_q%d" % n, [P, C], U32) for n in range(FEATURE_GROUPS)]
+        coef_s = [kept("coef_s%d" % n, [P, C], U8) for n in range(FEATURE_GROUPS)]
+        lab_sb = [kept("lab_sb%d" % n, [P, SLOTS, C], BF16) for n in range(ROW_GROUPS)]
+        lw_sb = [kept("lw_sb%d" % n, [P, SLOTS, C], BF16) for n in range(ROW_GROUPS)]
+        e_q = [kept("e_q%d" % n, [P, C], U32) for n in range(ROW_GROUPS)]
+        e_s = [kept("e_s%d" % n, [P, C], U8) for n in range(ROW_GROUPS)]
+        carry_sb = [kept("carry_sb%d" % n, [P, SLOTS, C], BF16) for n in range(FEATURE_GROUPS)]
+        y_sb = [kept("y_sb%d" % n, [P, SLOTS, C], F32) for n in range(FEATURE_GROUPS)]
+        y_q = [kept("y_q%d" % n, [P, C], U32) for n in range(FEATURE_GROUPS)]
+        y_s = kept("y_s", [P, FEATURE_GROUPS, C], U8)
+        direct_sb = kept("direct_sb", [P, FEATURE_GROUPS, WORD4 * GROUP], U8)
+        direct_sc = kept("direct_sc", [P, FEATURE_GROUPS, GROUP], U8)
+        direct_e = kept("direct_e", [P, SLOTS, C], BF16)
+        last_packed = kept("last_packed", [P, HALF, SLOTS], BF16)
+        w_bf = kept("w_bf", [P, ROW_GROUPS, SLOTS], BF16)
+        w_f32 = kept("w_f32", [P, ROW_GROUPS, SLOTS], F32)
+        d_bf = kept("d_bf", [P, FEATURE_GROUPS, SLOTS], BF16)
+        d_f32 = kept("d_f32", [P, FEATURE_GROUPS, SLOTS], F32)
+        ident = kept("ident", [P, P], F32)
+        warm = kept("warm", [P, 1], F32)
+
         sums = {}
-        turned_src = {}
+        emptied = {}
         turned = {}
-        flat = {}
-        grouped = {}
+        by_slot = {}
+        packed = {}
 
-        def logit_pass(h, g, i, dg):
-            rp, lo = divmod(g, 2)
-            nc.tensor.matmul_mx(
-                out=sums[("e", h, g, i)][:],
-                lhsT=coef_q[dg][:, c_tile(h, i)].bitcast(FP8X4),
-                lhsT_scale=coef_s[dg][:, c_tile(h, i)],
-                rhs=a_sb[rp][:, dg, 2 * GROUP * lo : 2 * GROUP * (lo + 1)].bitcast(FP4X4),
-                rhs_scale=a_sc[rp][:, dg, GROUP * lo : GROUP * (lo + 1)],
-                start=(dg == 0),
-                stop=(dg == DG - 1),
+        a_by_p = a_words.rearrange("g p n -> p g n")
+        f_by_p = f_words.rearrange("g p n -> p g n")
+
+        def load_rows(dst, src, g):
+            nc.sync.dma_start(out=dst[g][:], in_=src[g * GROUP : (g + 1) * GROUP, :].rearrange("(p t) c -> p t c", t=SLOTS))
+
+        def load_scale_rows(plane, rows):
+            by_r = rows.rearrange("g (q r) n -> r q g n", r=SCALE_RUN)
+            for r in range(SCALE_RUN):
+                nc.sync.dma_start(out=plane[r:P:QUADRANT, :, :].bitcast(I32), in_=by_r[r].bitcast(I32))
+
+        def load_a_early(k):
+            nc.sync.dma_start(out=a_sb[0][:, k, :].bitcast(I32), in_=a_by_p[:, k, 0 : WORD4 * EARLY_ROWS].bitcast(I32))
+
+        def load_a_late(g):
+            lo = WORD4 * (GROUP * g - EARLY_ROWS)
+            nc.sync.dma_start(
+                out=a_sb[1][:, :, lo : lo + WORD4 * GROUP].bitcast(I32),
+                in_=a_by_p[:, :, WORD4 * GROUP * g : WORD4 * GROUP * (g + 1)].bitcast(I32),
             )
 
-        def grad_pass(h, dg, i, g):
-            nc.tensor.matmul_mx(
-                out=sums[("y", h, dg, i)][:],
-                lhsT=e_q[g][:, c_tile(h, i)].bitcast(FP8X4),
-                lhsT_scale=e_s[g][:, c_tile(h, i)],
-                rhs=f_sb[dg][:, g, :].bitcast(FP4X4),
-                rhs_scale=f_sc[:, g, GROUP * dg : GROUP * (dg + 1)],
-                start=(g == 0),
-                stop=(g == RG - 1),
+        def load_f(g):
+            nc.sync.dma_start(
+                out=f_sb[g][:].bitcast(I32), in_=f_by_p[:, :, WORD4 * GROUP * g : WORD4 * GROUP * (g + 1)].bitcast(I32)
             )
 
-        def multiply(kind, h, g, banks, pass_major=False):
-            one, n = (logit_pass, DG) if kind == "e" else (grad_pass, RG)
-            keys = [(gg, i) for gg in g for i in range(2)]
-            for (gg, i), b in zip(keys, banks):
-                sums[(kind, h, gg, i)] = bank(b)
-            if pass_major:
-                for k in range(n):
-                    for gg, i in keys:
-                        one(h, gg, i, k)
-            else:
-                for gg, i in keys:
-                    for k in range(n):
-                        one(h, gg, i, k)
+        def load_factors():
+            nc.sync.dma_start(out=w_bf[:], in_=row_weight.rearrange("(g p t) -> p g t", p=P, t=SLOTS))
+            nc.sync.dma_start(out=d_bf[:], in_=diag.rearrange("(g p t) -> p g t", p=P, t=SLOTS))
+            nc.gpsimd.tensor_copy(out=w_f32[:], in_=w_bf[:])
+            nc.gpsimd.tensor_copy(out=d_f32[:], in_=d_bf[:])
+
+        def side_by_side(copy, dst, src):
+            copy(out=dst.rearrange("p (c i) t -> p c t i", i=4), in_=src.rearrange("p t (c i) -> p c t i", i=4))
+
+        def quantize(codes, scales, src):
+            nc.vector.quantize_mx(out=codes.bitcast(FP8X4), scales=scales, in_=src.rearrange("p c t -> p (c t)"))
+
+        def coef_pack(k, cols, copy):
+            side_by_side(copy, coef_packed[k][:, cols, :], coef_sb[k][:, :, cols])
+
+        def coef_quantize(k, cols):
+            quantize(coef_q[k][:, cols], coef_s[k][:, cols], coef_packed[k][:, cols, :])
+
+        def weigh_labels(g):
+            for t in range(SLOTS):
+                nc.vector.tensor_scalar(
+                    out=lw_sb[g][:, t, :], in0=lab_sb[g][:, t, :], scalar1=w_f32[:, g, t : t + 1], scalar2=None, op0=ALU.mult
+                )
+
+        def scale_carry(g):
+            for t in range(SLOTS):
+                nc.scalar.activation(
+                    out=y_sb[g][:, t, :], in_=carry_sb[g][:, t, :], func=ACT.Copy, scale=d_f32[:, g, t : t + 1]
+                )
+
+        def errors_slot(dst, prob, g, t, cols):
+            nc.vector.scalar_tensor_tensor(
+                out=dst, in0=prob, scalar=w_f32[:, g, t : t + 1], in1=lw_sb[g][:, t, cols], op0=ALU.mult, op1=ALU.subtract
+            )
+
+        def outputs_slot(grad, g, t, cols):
+            nc.vector.scalar_tensor_tensor(
+                out=y_sb[g][:, t, cols], in0=grad, scalar=d_f32[:, g, t : t + 1], in1=y_sb[g][:, t, cols],
+                op0=ALU.mult, op1=ALU.add,
+            )
+
+        def multiply(kind, h, g, i, passes):
+            key = (kind, h, g, i)
+            cols = targets(h, i)
+            for k in passes:
+                if k == 0:
+                    sums[key] = take_bank(key)
+                if kind == ERR:
+                    n, lo = divmod(GROUP * g, EARLY_ROWS)
+                    codes, scales, count = coef_q[k], coef_s[k], FEATURE_GROUPS
+                    words, word_scales = a_sb[n][:, k, WORD4 * lo : WORD4 * (lo + GROUP)], a_sc[n][:, k, lo : lo + GROUP]
+                else:
+                    codes, scales, count = e_q[k], e_s[k], ROW_GROUPS
+                    words, word_scales = f_sb[g][:, k, :], f_sc[:, k, GROUP * g : GROUP * (g + 1)]
+                nc.tensor.matmul_mx(
+                    out=sums[key][:],
+                    lhsT=codes[:, cols].bitcast(FP8X4),
+                    lhsT_scale=scales[:, cols],
+                    rhs=words.bitcast(FP4X4),
+                    rhs_scale=word_scales,
+                    start=(k == 0),
+                    stop=(k == count - 1),
+                )
+
+        def multiply_both(kind, h, g, passes):
+            for k in passes:
+                multiply(kind, h, g, 0, [k])
+                multiply(kind, h, g, 1, [k])
+
+        def staging():
+            return work.tile([P, SLOTS, P], F32, name="staging", bufs=12)
 
         def empty(kind, h, g, i):
-            src = sums[(kind, h, g, i)][:].rearrange("c (p t) -> c t p", t=PACK)
-            dst = work.tile([P, PACK, P], F32, name="turn_src", bufs=8)
-            turned_src[(kind, h, g, i)] = dst
-            if kind == "e":
-                nc.scalar.activation(out=dst[:], in_=src, func=ACT.Sigmoid)
+            key = (kind, h, g, i)
+            src = sums[key][:].rearrange("c (p t) -> c t p", t=SLOTS)
+            emptied[key] = staging()
+            if kind == ERR:
+                nc.scalar.activation(out=emptied[key][:], in_=src, func=ACT.Sigmoid)
             else:
-                nc.scalar.copy(out=dst[:], in_=src)
+                nc.scalar.copy(out=emptied[key][:], in_=src)
+            give_bank(key)
 
-        def turn(kind, h, g, banks):
-            pair = [bank(b) for b in banks]
+        def turn(kind, h, g):
+            pair = [take_bank((kind, h, g, "turned", u)) for u in range(2)]
             turned[(kind, h, g)] = pair
             for i in range(2):
-                for t in range(PACK):
+                for t in range(SLOTS):
                     lo = HALF * (t % 2) + P * i
-                    nc.tensor.transpose(pair[t // 2][:, lo : lo + P], turned_src[(kind, h, g, i)][:, t, :], ident[:])
+                    nc.tensor.transpose(pair[t // 2][:, lo : lo + P], emptied[(kind, h, g, i)][:, t, :], ident[:])
 
         def combine(kind, h, g):
             pair = turned[(kind, h, g)]
-            if kind == "e":
-                dst = work.tile([P, PACK, HALF], BF16, name="e_flat", bufs=3)
-                flat[(kind, h, g)] = dst[:]
+            if kind == ERR:
+                e_by_slot = work.tile([P, SLOTS, HALF], BF16, name="e_by_slot", bufs=4)
+                by_slot[(kind, h, g)] = e_by_slot[:]
             else:
-                flat[(kind, h, g)] = y_sb[g][:, :, half(h)]
-            for t in range(PACK):
+                by_slot[(kind, h, g)] = y_sb[g][:, :, half(h)]
+            for t in range(SLOTS):
                 src = pair[t // 2][:, HALF * (t % 2) : HALF * (t % 2 + 1)]
-                if kind == "e":
-                    nc.vector.scalar_tensor_tensor(
-                        out=dst[:, t, :], in0=src, scalar=w_f32[:, g, t : t + 1], in1=lw_sb[g][:, t, half(h)],
-                        op0=ALU.mult, op1=ALU.subtract,
-                    )
+                if kind == ERR:
+                    errors_slot(by_slot[(kind, h, g)][:, t, :], src, g, t, half(h))
                 else:
-                    nc.vector.scalar_tensor_tensor(
-                        out=y_sb[g][:, t, half(h)], in0=src, scalar=d_f32[:, g, t : t + 1], in1=y_sb[g][:, t, half(h)],
-                        op0=ALU.mult, op1=ALU.add,
-                    )
-            if kind == "y":
-                nc.sync.dma_start(
-                    out=out_0[g * GROUP : (g + 1) * GROUP, half(h)].rearrange("(p t) c -> p t c", t=PACK),
-                    in_=y_sb[g][:, :, half(h)],
-                )
+                    outputs_slot(src, g, t, half(h))
+                if t % 2:
+                    give_bank((kind, h, g, "turned", t // 2))
 
-        def group(kind, h, g, engine_copy):
-            dst = work.tile([P, HALF, PACK], BF16, name="grouped", bufs=3, align_bytes=64)
-            grouped[(kind, h, g)] = dst
-            interleave(engine_copy, dst[:], flat[(kind, h, g)])
+        def pack(kind, h, g, copy):
+            packed[(kind, h, g)] = work.tile([P, HALF, SLOTS], BF16, name="packed", bufs=4, align_bytes=64)
+            side_by_side(copy, packed[(kind, h, g)][:], by_slot[(kind, h, g)])
 
         def finish(kind, h, g):
-            if kind == "e":
-                quantize(e_q[g][:, half(h)], e_s[g][:, half(h)], grouped[(kind, h, g)][:])
+            if kind == ERR:
+                quantize(e_q[g][:, half(h)], e_s[g][:, half(h)], packed[(kind, h, g)][:])
             else:
-                quantize(y_q[g][:, half(h)], y_s[:, g, half(h)], grouped[(kind, h, g)][:])
-                nc.sync.dma_start(
-                    out=out_1[g].rearrange("p c t -> p (c t)")[:, PACK * HALF * h : PACK * HALF * (h + 1)].bitcast(I32),
-                    in_=y_q[g][:, half(h)].bitcast(I32),
-                )
+                quantize(y_q[g][:, half(h)], y_s[:, g, half(h)], packed[(kind, h, g)][:])
 
-        LO, HI = [0, 1, 2, 3], [4, 5, 6, 7]
-        V, S = nc.vector.tensor_copy, nc.scalar.copy
+        direct_lo = GROUP * DIRECT - EARLY_ROWS
 
-        multiply("e", 0, [0, 1], LO, pass_major=True)
-        label_weights(0)
-        label_weights(1)
-        for g in (0, 1):
-            for i in range(2):
-                empty("e", 0, g, i)
-        multiply("e", 0, [2, 3], HI)
-        for g in (2, 3):
-            for i in range(2):
-                empty("e", 0, g, i)
-
-        rounds = [
-            ([("e", 0, 0), ("e", 0, 1)], [("e", 1, 0), ("e", 1, 1)]),
-            ([("e", 0, 2), ("e", 0, 3)], [("e", 1, 2), ("e", 1, 3)]),
-            ([("e", 1, 0), ("e", 1, 1)], [("y", 0, 0), ("y", 0, 1)]),
-        ]
-        for n, (old, new) in enumerate(rounds):
-            turn(*old[0], LO[:2])
-            turn(*old[1], LO[2:])
-            multiply(new[0][0], new[0][1], [new[0][2], new[1][2]], HI)
-            combine(*old[0])
-            combine(*old[1])
-            empty(*new[0], 0)
-            group(*old[0], S)
-            empty(*new[0], 1)
-            empty(*new[1], 0)
-            empty(*new[1], 1)
-            if n == 0:
-                label_weights(2)
-                label_weights(3)
-            group(*old[1], V)
-            finish(*old[0])
-            finish(*old[1])
-        carry_diag(0)
-
-        turn("e", 1, 2, LO[:2])
-        turn("e", 1, 3, LO[2:])
-        multiply("y", 0, [2], HI[:2])
-        combine("e", 1, 2)
-        combine("e", 1, 3)
-        group("e", 1, 2, S)
-        empty("y", 0, 2, 0)
-        empty("y", 0, 2, 1)
-        carry_diag(1)
-        group("e", 1, 3, V)
-        finish("e", 1, 2)
-        finish("e", 1, 3)
-
-        turn("y", 0, 0, LO[:2])
-        turn("y", 0, 1, LO[2:])
-        multiply("y", 1, [0], HI[2:], pass_major=True)
-        multiply("y", 1, [1], HI[:2])
-        combine("y", 0, 0)
-        combine("y", 0, 1)
-        empty("y", 1, 0, 0)
-        empty("y", 1, 0, 1)
-        carry_diag(2)
-        empty("y", 1, 1, 0)
-        empty("y", 1, 1, 1)
-        group("y", 0, 0, V)
-        group("y", 0, 1, V)
-        finish("y", 0, 0)
-        finish("y", 0, 1)
-
-        def last_multiply(i):
-            sums[("y", 1, 2, i)] = bank(HI[2 + i])
-            for k in range(RG):
-                grad_pass(1, 2, i, k)
-
-        def last_turn(i):
-            dst = bank(LO[2 + i])
-            turned[("last", i)] = dst
-            for t in range(PACK):
-                nc.tensor.transpose(dst[:, P * t : P * (t + 1)], turned_src[("y", 1, 2, i)][:, t, :], ident[:])
-
-        def last_combine(i):
-            cols = c_tile(1, i)
-            for t in range(PACK):
-                nc.vector.scalar_tensor_tensor(
-                    out=y_sb[2][:, t, cols], in0=turned[("last", i)][:, P * t : P * (t + 1)], scalar=d_f32[:, 2, t : t + 1],
-                    in1=y_sb[2][:, t, cols], op0=ALU.mult, op1=ALU.add,
-                )
-            nc.sync.dma_start(
-                out=out_0[2 * GROUP :, cols].rearrange("(p t) c -> p t c", t=PACK), in_=y_sb[2][:, :, cols]
+        def reorder_words(k):
+            nc.vector.tensor_copy(
+                out=direct_sb[:, k, :].rearrange("p (t m b) -> p t m b", t=SLOTS, b=WORD4),
+                in_=a_sb[1][:, k, WORD4 * direct_lo : WORD4 * (direct_lo + GROUP)].rearrange(
+                    "p (m t b) -> p t m b", t=SLOTS, b=WORD4
+                ),
             )
 
-        def last_group(i, engine_copy):
-            dst = work.tile([P, P, PACK], BF16, name="last_grouped", bufs=2, align_bytes=64)
-            grouped[("last", i)] = dst
-            interleave(engine_copy, dst[:], y_sb[2][:, :, c_tile(1, i)])
+        def reorder_scales():
+            nc.vector.tensor_copy(
+                out=direct_sc[:].rearrange("p g (t m) -> p g t m", t=SLOTS),
+                in_=a_sc[1][:, :, direct_lo : direct_lo + GROUP].rearrange("p g (m t) -> p g t m", t=SLOTS),
+            )
+
+        def direct_multiply(t):
+            sums[("direct", t)] = take_bank(("direct", t))
+            for k in range(FEATURE_GROUPS):
+                nc.tensor.matmul_mx(
+                    out=sums[("direct", t)][:],
+                    lhsT=direct_sb[:, k, WORD4 * P * t : WORD4 * P * (t + 1)].bitcast(FP4X4),
+                    lhsT_scale=direct_sc[:, k, P * t : P * (t + 1)],
+                    rhs=coef_q[k][:].bitcast(FP8X4),
+                    rhs_scale=coef_s[k][:],
+                    start=(k == 0),
+                    stop=(k == FEATURE_GROUPS - 1),
+                )
+
+        def direct_empty(t):
+            emptied[("direct", t)] = staging()
+            nc.scalar.activation(
+                out=emptied[("direct", t)][:].rearrange("p a b -> p (a b)"), in_=sums[("direct", t)][:], func=ACT.Sigmoid
+            )
+            give_bank(("direct", t))
+
+        def direct_combine(t):
+            errors_slot(direct_e[:, t, :], emptied[("direct", t)][:].rearrange("p a b -> p (a b)"), DIRECT, t, slice(0, C))
+
+        for h in range(2):
+            by_slot[(ERR, h, DIRECT)] = direct_e[:, :, half(h)]
+
+        def last_turn(i):
+            turned[("last", i)] = take_bank(("last", i))
+            for t in range(SLOTS):
+                nc.tensor.transpose(
+                    turned[("last", i)][:, P * t : P * (t + 1)], emptied[(OUT, 1, LAST, i)][:, t, :], ident[:]
+                )
+
+        def last_combine(i):
+            for t in range(SLOTS):
+                outputs_slot(turned[("last", i)][:, P * t : P * (t + 1)], LAST, t, targets(1, i))
+            give_bank(("last", i))
+
+        def last_pack(i, copy):
+            side_by_side(copy, last_packed[:, targets(0, i), :], y_sb[LAST][:, :, targets(1, i)])
 
         def last_finish(i):
-            cols = c_tile(1, i)
-            quantize(y_q[2][:, cols], y_s[:, 2, cols], grouped[("last", i)][:])
+            quantize(y_q[LAST][:, targets(1, i)], y_s[:, LAST, targets(1, i)], last_packed[:, targets(0, i), :])
 
-        turn("y", 0, 2, LO[:2])
-        turn("y", 1, 0, LO[2:])
-        last_multiply(0)
-        combine("y", 0, 2)
-        combine("y", 1, 0)
-        group("y", 0, 2, S)
-        empty("y", 1, 2, 0)
-        turn("y", 1, 1, LO[:2])
-        last_multiply(1)
-        empty("y", 1, 2, 1)
+        def store_y(g, cols):
+            nc.sync.dma_start(
+                out=out_0[g * GROUP : (g + 1) * GROUP, cols].rearrange("(p t) c -> p t c", t=SLOTS), in_=y_sb[g][:, :, cols]
+            )
+
+        def store_codes(g, h, queue):
+            queue.dma_start(
+                out=out_1[g].rearrange("p c t -> p (c t)")[:, SLOTS * HALF * h : SLOTS * HALF * (h + 1)].bitcast(I32),
+                in_=y_q[g][:, half(h)].bitcast(I32),
+            )
+
+        for plane in a_sc:
+            nc.vector.memset(plane[:].bitcast(I32), 0)
+        nc.vector.memset(warm[:], 0.0)
+        make_identity(nc, ident[:])
+        nc.gpsimd.memset(f_sc[:].bitcast(I32), 0)
+        nc.scalar.activation(out=warm[:], in_=warm[:], func=ACT.Sigmoid)
+
+        load_rows(coef_sb, coef, 0)
+        load_a_early(0)
+        load_scale_rows(a_sc[0], a_scales[:, :, 0:EARLY_ROWS])
+        load_rows(coef_sb, coef, 1)
+        load_a_early(1)
+        load_rows(coef_sb, coef, 2)
+        load_a_late(2)
+        load_a_early(2)
+        load_scale_rows(a_sc[1], a_scales[:, :, EARLY_ROWS:])
+        load_factors()
+        load_rows(lab_sb, labels, 0)
+        load_rows(lab_sb, labels, 1)
+        load_rows(lab_sb, labels, 2)
+        load_a_late(3)
+        load_rows(lab_sb, labels, 3)
+        load_scale_rows(f_sc, f_scales)
+        load_f(0)
+        load_rows(carry_sb, carry, 0)
+        load_f(1)
+        load_rows(carry_sb, carry, 1)
+        load_f(2)
+        load_rows(carry_sb, carry, 2)
+
+        coef_pack(0, targets(0, 0), on_vector)
+        coef_pack(0, half(1), on_scalar)
+        coef_pack(0, targets(0, 1), on_vector)
+        coef_quantize(0, targets(0, 0))
+        coef_quantize(0, targets(0, 1))
+        multiply_both(ERR, 0, 0, [0])
+        multiply_both(ERR, 0, 1, [0])
+        coef_quantize(0, half(1))
+        multiply_both(ERR, 1, 0, [0])
+        multiply_both(ERR, 1, 1, [0])
+        coef_pack(1, targets(0, 0), on_vector)
+        coef_pack(1, half(1), on_scalar)
+        coef_pack(1, targets(0, 1), on_vector)
+        coef_quantize(1, targets(0, 0))
+        coef_quantize(1, targets(0, 1))
+        coef_quantize(1, half(1))
+        multiply_both(ERR, 0, 0, [1])
+        multiply_both(ERR, 0, 1, [1])
+        multiply_both(ERR, 1, 0, [1])
+        multiply_both(ERR, 1, 1, [1])
+        coef_pack(2, targets(0, 0), on_vector)
+        coef_pack(2, half(1), on_scalar)
+        coef_pack(2, targets(0, 1), on_vector)
+        coef_quantize(2, targets(0, 0))
+        coef_quantize(2, targets(0, 1))
+        reorder_words(0)
+        coef_quantize(2, half(1))
+        reorder_words(1)
+        reorder_scales()
+        reorder_words(2)
+        multiply_both(ERR, 0, 0, [2])
+        empty(ERR, 0, 0, 0)
+        empty(ERR, 0, 0, 1)
+        multiply_both(ERR, 0, 1, [2])
+        multiply_both(ERR, 1, 0, [2])
+        empty(ERR, 0, 1, 0)
+        empty(ERR, 0, 1, 1)
+        turn(ERR, 0, 0)
+        multiply_both(ERR, 1, 1, [2])
+        weigh_labels(0)
+        empty(ERR, 1, 0, 0)
+        empty(ERR, 1, 0, 1)
+        combine(ERR, 0, 0)
+        direct_multiply(0)
+        direct_multiply(1)
+        weigh_labels(1)
+        weigh_labels(2)
+        direct_empty(0)
+        empty(ERR, 1, 1, 0)
+        direct_empty(1)
+        turn(ERR, 0, 1)
+        direct_multiply(2)
+        direct_multiply(3)
+        weigh_labels(3)
+        pack(ERR, 0, 0, on_scalar)
+        direct_combine(0)
+        combine(ERR, 0, 1)
+        direct_empty(2)
+        empty(ERR, 1, 1, 1)
+        direct_empty(3)
+        multiply(ERR, 0, 3, 0, range(FEATURE_GROUPS))
+        multiply(ERR, 0, 3, 1, range(FEATURE_GROUPS))
+        finish(ERR, 0, 0)
+        direct_combine(1)
+        pack(ERR, 0, 1, on_vector)
+        multiply(ERR, 1, 3, 0, range(FEATURE_GROUPS))
+        empty(ERR, 0, 3, 0)
+        empty(ERR, 0, 3, 1)
+        multiply(ERR, 1, 3, 1, range(FEATURE_GROUPS))
+        direct_combine(2)
+        direct_combine(3)
+        finish(ERR, 0, 1)
+        empty(ERR, 1, 3, 0)
+        empty(ERR, 1, 3, 1)
+        turn(ERR, 0, 3)
+        turn(ERR, 1, 0)
+        turn(ERR, 1, 1)
+        pack(ERR, 0, 2, on_vector)
+        pack(ERR, 1, 2, on_scalar)
+        combine(ERR, 0, 3)
+        multiply_both(OUT, 0, 0, [0, 1])
+        scale_carry(0)
+        finish(ERR, 0, 2)
+        pack(ERR, 0, 3, on_vector)
+        multiply_both(OUT, 0, 1, [0, 1])
+        finish(ERR, 0, 3)
+        combine(ERR, 1, 0)
+        multiply_both(OUT, 0, 0, [2, 3])
+        multiply_both(OUT, 0, 1, [2, 3])
+        empty(OUT, 0, 0, 0)
+        empty(OUT, 0, 0, 1)
+        combine(ERR, 1, 1)
+        turn(ERR, 1, 3)
+        empty(OUT, 0, 1, 0)
+        empty(OUT, 0, 1, 1)
+        pack(ERR, 1, 0, on_vector)
+        multiply(OUT, 0, 2, 0, range(ROW_GROUPS))
+        multiply(OUT, 0, 2, 1, range(ROW_GROUPS))
+        finish(ERR, 1, 2)
+        finish(ERR, 1, 0)
+        scale_carry(1)
+        combine(ERR, 1, 3)
+        pack(ERR, 1, 1, on_vector)
+        pack(ERR, 1, 3, on_vector)
+        turn(OUT, 0, 0)
+        turn(OUT, 0, 1)
+        empty(OUT, 0, 2, 0)
+        empty(OUT, 0, 2, 1)
+        finish(ERR, 1, 1)
+        finish(ERR, 1, 3)
+        turn(OUT, 0, 2)
+        scale_carry(2)
+        combine(OUT, 0, 0)
+        multiply_both(OUT, 1, 0, range(ROW_GROUPS))
+        store_y(0, half(0))
+        combine(OUT, 0, 1)
+        store_y(1, half(0))
+        combine(OUT, 0, 2)
+        store_y(2, half(0))
+        multiply(OUT, 1, 1, 0, range(ROW_GROUPS))
+        empty(OUT, 1, 0, 0)
+        empty(OUT, 1, 0, 1)
+        turn(OUT, 1, 0)
+        pack(OUT, 0, 0, on_vector)
+        empty(OUT, 1, 1, 0)
+        multiply(OUT, 1, 1, 1, range(ROW_GROUPS))
+        pack(OUT, 0, 1, on_scalar)
+        combine(OUT, 1, 0)
+        multiply(OUT, 1, 2, 0, range(ROW_GROUPS))
+        pack(OUT, 0, 2, on_vector)
+        empty(OUT, 1, 1, 1)
+        store_y(0, half(1))
+        finish(OUT, 0, 0)
+        turn(OUT, 1, 1)
+        finish(OUT, 0, 1)
+        empty(OUT, 1, 2, 0)
+        finish(OUT, 0, 2)
+        store_codes(0, 0, nc.sync)
+        store_codes(1, 0, nc.sync)
+        store_codes(2, 0, nc.sync)
+        pack(OUT, 1, 0, on_scalar)
+        combine(OUT, 1, 1)
         last_turn(0)
-        last_turn(1)
-        group("y", 1, 0, S)
-        combine("y", 1, 1)
-        finish("y", 0, 2)
-        group("y", 1, 1, S)
+        multiply(OUT, 1, 2, 1, range(ROW_GROUPS))
         last_combine(0)
-        finish("y", 1, 0)
+        store_y(1, half(1))
+        pack(OUT, 1, 1, on_vector)
+        empty(OUT, 1, 2, 1)
+        store_y(LAST, targets(1, 0))
+        last_pack(0, on_scalar)
+        finish(OUT, 1, 0)
+        last_turn(1)
+        finish(OUT, 1, 1)
+        store_codes(0, 1, nc.sync)
+        store_codes(1, 1, nc.sync)
         last_combine(1)
-        last_group(0, V)
-        last_group(1, V)
-        finish("y", 1, 1)
+        last_pack(1, on_vector)
+        store_y(LAST, targets(1, 1))
         last_finish(0)
         last_finish(1)
-        nc.scalar.dma_start(
-            out=out_1[2].rearrange("p c t -> p (c t)")[:, PACK * HALF :].bitcast(I32), in_=y_q[2][:, HALF:].bitcast(I32)
-        )
+        store_codes(2, 1, nc.scalar)
 
-        by_r = out_2.rearrange("g (q r) c -> r q g c", r=4)
-        for r in range(4):
+        by_r = out_2.rearrange("g (q r) c -> r q g c", r=SCALE_RUN)
+        for r in range(SCALE_RUN):
             queue = nc.scalar if r % 2 else nc.sync
-            queue.dma_start(out=by_r[r].bitcast(I32), in_=y_s[r:P:32, :, :].bitcast(I32))
+            queue.dma_start(out=by_r[r].bitcast(I32), in_=y_s[r:P:QUADRANT, :, :].bitcast(I32))

@@ -62,7 +62,8 @@ def tile_preconditioned_logistic_gradient_h1_kernel(
         def targets(h, i):
             return slice(HALF * h + P * i, HALF * h + P * (i + 1))
 
-        a_sb = [kept("a_sb%d" % n, [P, FEATURE_GROUPS, WORD4 * EARLY_ROWS], U8) for n in range(2)]
+        a_early = kept("a_early", [P, FEATURE_GROUPS, WORD4 * EARLY_ROWS], U8)
+        a_late = {g: kept("a_late%d" % g, [P, FEATURE_GROUPS, WORD4 * GROUP], U8) for g in range(2, ROW_GROUPS)}
         a_sc = [kept("a_sc%d" % n, [P, FEATURE_GROUPS, EARLY_ROWS], U8) for n in range(2)]
         f_sb = [kept("f_sb%d" % n, [P, ROW_GROUPS, WORD4 * GROUP], U8) for n in range(FEATURE_GROUPS)]
         f_sc = kept("f_sc", [P, ROW_GROUPS, D], U8)
@@ -75,7 +76,8 @@ def tile_preconditioned_logistic_gradient_h1_kernel(
         e_q = [kept("e_q%d" % n, [P, C], U32) for n in range(ROW_GROUPS)]
         e_s = [kept("e_s%d" % n, [P, C], U8) for n in range(ROW_GROUPS)]
         carry_sb = [kept("carry_sb%d" % n, [P, SLOTS, C], BF16) for n in range(FEATURE_GROUPS)]
-        y_sb = [kept("y_sb%d" % n, [P, SLOTS, C], F32) for n in range(FEATURE_GROUPS)]
+        y_sb = [kept("y_sb%d" % n, [P, SLOTS, HALF if n == LAST else C], F32) for n in range(FEATURE_GROUPS)]
+        y_last = kept("y_last", [P, 2, SLOTS, P], F32)
         y_q = [kept("y_q%d" % n, [P, C], U32) for n in range(FEATURE_GROUPS)]
         y_s = kept("y_s", [P, FEATURE_GROUPS, C], U8)
         direct_sb = kept("direct_sb", [P, FEATURE_GROUPS, WORD4 * GROUP], U8)
@@ -107,13 +109,11 @@ def tile_preconditioned_logistic_gradient_h1_kernel(
                 nc.sync.dma_start(out=plane[r:P:QUADRANT, :, :].bitcast(I32), in_=by_r[r].bitcast(I32))
 
         def load_a_early(k):
-            nc.sync.dma_start(out=a_sb[0][:, k, :].bitcast(I32), in_=a_by_p[:, k, 0 : WORD4 * EARLY_ROWS].bitcast(I32))
+            nc.sync.dma_start(out=a_early[:, k, :].bitcast(I32), in_=a_by_p[:, k, 0 : WORD4 * EARLY_ROWS].bitcast(I32))
 
         def load_a_late(g):
-            lo = WORD4 * (GROUP * g - EARLY_ROWS)
             nc.sync.dma_start(
-                out=a_sb[1][:, :, lo : lo + WORD4 * GROUP].bitcast(I32),
-                in_=a_by_p[:, :, WORD4 * GROUP * g : WORD4 * GROUP * (g + 1)].bitcast(I32),
+                out=a_late[g][:].bitcast(I32), in_=a_by_p[:, :, WORD4 * GROUP * g : WORD4 * GROUP * (g + 1)].bitcast(I32)
             )
 
         def load_f(g):
@@ -147,20 +147,21 @@ def tile_preconditioned_logistic_gradient_h1_kernel(
 
         def scale_carry(g):
             for t in range(SLOTS):
-                nc.scalar.activation(
-                    out=y_sb[g][:, t, :], in_=carry_sb[g][:, t, :], func=ACT.Copy, scale=d_f32[:, g, t : t + 1]
-                )
+                if g == LAST:
+                    last_carry = carry_sb[g][:, t, half(1)].rearrange("p (i c) -> p i c", i=2)
+                    parts = [(y_sb[g][:, t, :], carry_sb[g][:, t, half(0)]), (y_last[:, :, t, :], last_carry)]
+                else:
+                    parts = [(y_sb[g][:, t, :], carry_sb[g][:, t, :])]
+                for dst, src in parts:
+                    nc.scalar.activation(out=dst, in_=src, func=ACT.Copy, scale=d_f32[:, g, t : t + 1])
 
         def errors_slot(dst, prob, g, t, cols):
             nc.vector.scalar_tensor_tensor(
                 out=dst, in0=prob, scalar=w_f32[:, g, t : t + 1], in1=lw_sb[g][:, t, cols], op0=ALU.mult, op1=ALU.subtract
             )
 
-        def outputs_slot(grad, g, t, cols):
-            nc.vector.scalar_tensor_tensor(
-                out=y_sb[g][:, t, cols], in0=grad, scalar=d_f32[:, g, t : t + 1], in1=y_sb[g][:, t, cols],
-                op0=ALU.mult, op1=ALU.add,
-            )
+        def outputs_slot(y, grad, g, t):
+            nc.vector.scalar_tensor_tensor(out=y, in0=grad, scalar=d_f32[:, g, t : t + 1], in1=y, op0=ALU.mult, op1=ALU.add)
 
         def multiply(kind, h, g, i, passes):
             key = (kind, h, g, i)
@@ -171,7 +172,8 @@ def tile_preconditioned_logistic_gradient_h1_kernel(
                 if kind == ERR:
                     n, lo = divmod(GROUP * g, EARLY_ROWS)
                     codes, scales, count = coef_q[k], coef_s[k], FEATURE_GROUPS
-                    words, word_scales = a_sb[n][:, k, WORD4 * lo : WORD4 * (lo + GROUP)], a_sc[n][:, k, lo : lo + GROUP]
+                    words = a_late[g][:, k, :] if n else a_early[:, k, WORD4 * lo : WORD4 * (lo + GROUP)]
+                    word_scales = a_sc[n][:, k, lo : lo + GROUP]
                 else:
                     codes, scales, count = e_q[k], e_s[k], ROW_GROUPS
                     words, word_scales = f_sb[g][:, k, :], f_sc[:, k, GROUP * g : GROUP * (g + 1)]
@@ -223,7 +225,7 @@ def tile_preconditioned_logistic_gradient_h1_kernel(
                 if kind == ERR:
                     errors_slot(by_slot[(kind, h, g)][:, t, :], src, g, t, half(h))
                 else:
-                    outputs_slot(src, g, t, half(h))
+                    outputs_slot(by_slot[(kind, h, g)][:, t, :], src, g, t)
                 if t % 2:
                     give_bank((kind, h, g, "turned", t // 2))
 
@@ -242,9 +244,7 @@ def tile_preconditioned_logistic_gradient_h1_kernel(
         def reorder_words(k):
             nc.vector.tensor_copy(
                 out=direct_sb[:, k, :].rearrange("p (t m b) -> p t m b", t=SLOTS, b=WORD4),
-                in_=a_sb[1][:, k, WORD4 * direct_lo : WORD4 * (direct_lo + GROUP)].rearrange(
-                    "p (m t b) -> p t m b", t=SLOTS, b=WORD4
-                ),
+                in_=a_late[DIRECT][:, k, :].rearrange("p (m t b) -> p t m b", t=SLOTS, b=WORD4),
             )
 
         def reorder_scales():
@@ -288,19 +288,23 @@ def tile_preconditioned_logistic_gradient_h1_kernel(
 
         def last_combine(i):
             for t in range(SLOTS):
-                outputs_slot(turned[("last", i)][:, P * t : P * (t + 1)], LAST, t, targets(1, i))
+                outputs_slot(y_last[:, i, t, :], turned[("last", i)][:, P * t : P * (t + 1)], LAST, t)
             give_bank(("last", i))
 
         def last_pack(i, copy):
-            side_by_side(copy, last_packed[:, targets(0, i), :], y_sb[LAST][:, :, targets(1, i)])
+            side_by_side(copy, last_packed[:, targets(0, i), :], y_last[:, i, :, :])
 
         def last_finish(i):
             quantize(y_q[LAST][:, targets(1, i)], y_s[:, LAST, targets(1, i)], last_packed[:, targets(0, i), :])
 
-        def store_y(g, cols):
-            nc.sync.dma_start(
-                out=out_0[g * GROUP : (g + 1) * GROUP, cols].rearrange("(p t) c -> p t c", t=SLOTS), in_=y_sb[g][:, :, cols]
-            )
+        def store_rows(g, cols, src):
+            nc.sync.dma_start(out=out_0[g * GROUP : (g + 1) * GROUP, cols].rearrange("(p t) c -> p t c", t=SLOTS), in_=src)
+
+        def store_y(g, h):
+            store_rows(g, half(h), y_sb[g][:, :, half(h)])
+
+        def last_store(i):
+            store_rows(LAST, targets(1, i), y_last[:, i, :, :])
 
         def store_codes(g, h, queue):
             queue.dma_start(
@@ -316,19 +320,19 @@ def tile_preconditioned_logistic_gradient_h1_kernel(
         nc.scalar.activation(out=warm[:], in_=warm[:], func=ACT.Sigmoid)
 
         load_rows(coef_sb, coef, 0)
-        load_a_early(0)
         load_scale_rows(a_sc[0], a_scales[:, :, 0:EARLY_ROWS])
+        load_a_early(0)
         load_rows(coef_sb, coef, 1)
-        load_a_early(1)
         load_rows(coef_sb, coef, 2)
+        load_a_early(1)
         load_a_late(2)
         load_a_early(2)
         load_scale_rows(a_sc[1], a_scales[:, :, EARLY_ROWS:])
         load_factors()
         load_rows(lab_sb, labels, 0)
+        load_a_late(3)
         load_rows(lab_sb, labels, 1)
         load_rows(lab_sb, labels, 2)
-        load_a_late(3)
         load_rows(lab_sb, labels, 3)
         load_scale_rows(f_sc, f_scales)
         load_f(0)
@@ -338,164 +342,159 @@ def tile_preconditioned_logistic_gradient_h1_kernel(
         load_f(2)
         load_rows(carry_sb, carry, 2)
 
-        coef_pack(0, targets(0, 0), on_vector)
-        coef_pack(0, half(1), on_scalar)
-        coef_pack(0, targets(0, 1), on_vector)
-        coef_quantize(0, targets(0, 0))
-        coef_quantize(0, targets(0, 1))
+        coef_pack(0, half(0), on_vector)
+        coef_pack(0, targets(1, 0), on_scalar)
+        coef_quantize(0, half(0))
         multiply_both(ERR, 0, 0, [0])
         multiply_both(ERR, 0, 1, [0])
+        coef_pack(0, targets(1, 1), on_vector)
         coef_quantize(0, half(1))
         multiply_both(ERR, 1, 0, [0])
         multiply_both(ERR, 1, 1, [0])
-        coef_pack(1, targets(0, 0), on_vector)
+        coef_pack(1, half(0), on_vector)
         coef_pack(1, half(1), on_scalar)
-        coef_pack(1, targets(0, 1), on_vector)
-        coef_quantize(1, targets(0, 0))
-        coef_quantize(1, targets(0, 1))
+        coef_pack(2, half(0), on_vector)
+        coef_quantize(1, half(0))
         coef_quantize(1, half(1))
+        coef_pack(2, half(1), on_scalar)
+        coef_quantize(2, half(0))
         multiply_both(ERR, 0, 0, [1])
         multiply_both(ERR, 0, 1, [1])
         multiply_both(ERR, 1, 0, [1])
-        multiply_both(ERR, 1, 1, [1])
-        coef_pack(2, targets(0, 0), on_vector)
-        coef_pack(2, half(1), on_scalar)
-        coef_pack(2, targets(0, 1), on_vector)
-        coef_quantize(2, targets(0, 0))
-        coef_quantize(2, targets(0, 1))
         reorder_words(0)
         coef_quantize(2, half(1))
-        reorder_words(1)
-        reorder_scales()
-        reorder_words(2)
         multiply_both(ERR, 0, 0, [2])
         empty(ERR, 0, 0, 0)
         empty(ERR, 0, 0, 1)
         multiply_both(ERR, 0, 1, [2])
+        multiply_both(ERR, 1, 1, [1])
         multiply_both(ERR, 1, 0, [2])
+        multiply_both(ERR, 1, 1, [2])
+        reorder_scales()
+        reorder_words(1)
+        reorder_words(2)
         empty(ERR, 0, 1, 0)
         empty(ERR, 0, 1, 1)
         turn(ERR, 0, 0)
-        multiply_both(ERR, 1, 1, [2])
-        weigh_labels(0)
+        turn(ERR, 0, 1)
         empty(ERR, 1, 0, 0)
         empty(ERR, 1, 0, 1)
+        empty(ERR, 1, 1, 0)
+        empty(ERR, 1, 1, 1)
+        weigh_labels(0)
         combine(ERR, 0, 0)
         direct_multiply(0)
         direct_multiply(1)
         weigh_labels(1)
-        weigh_labels(2)
         direct_empty(0)
-        empty(ERR, 1, 1, 0)
-        direct_empty(1)
-        turn(ERR, 0, 1)
+        combine(ERR, 0, 1)
         direct_multiply(2)
         direct_multiply(3)
-        weigh_labels(3)
         pack(ERR, 0, 0, on_scalar)
+        weigh_labels(2)
+        direct_empty(1)
         direct_combine(0)
-        combine(ERR, 0, 1)
-        direct_empty(2)
-        empty(ERR, 1, 1, 1)
-        direct_empty(3)
+        finish(ERR, 0, 0)
         multiply(ERR, 0, 3, 0, range(FEATURE_GROUPS))
         multiply(ERR, 0, 3, 1, range(FEATURE_GROUPS))
-        finish(ERR, 0, 0)
+        direct_empty(2)
+        direct_empty(3)
         direct_combine(1)
-        pack(ERR, 0, 1, on_vector)
-        multiply(ERR, 1, 3, 0, range(FEATURE_GROUPS))
-        empty(ERR, 0, 3, 0)
-        empty(ERR, 0, 3, 1)
-        multiply(ERR, 1, 3, 1, range(FEATURE_GROUPS))
+        weigh_labels(3)
         direct_combine(2)
         direct_combine(3)
-        finish(ERR, 0, 1)
+        multiply(ERR, 1, 3, 0, range(FEATURE_GROUPS))
+        multiply(ERR, 1, 3, 1, range(FEATURE_GROUPS))
+        empty(ERR, 0, 3, 0)
+        empty(ERR, 0, 3, 1)
+        turn(ERR, 0, 3)
         empty(ERR, 1, 3, 0)
         empty(ERR, 1, 3, 1)
-        turn(ERR, 0, 3)
         turn(ERR, 1, 0)
         turn(ERR, 1, 1)
-        pack(ERR, 0, 2, on_vector)
-        pack(ERR, 1, 2, on_scalar)
+        pack(ERR, 0, 1, on_vector)
+        pack(ERR, 0, 2, on_scalar)
         combine(ERR, 0, 3)
-        multiply_both(OUT, 0, 0, [0, 1])
-        scale_carry(0)
-        finish(ERR, 0, 2)
+        finish(ERR, 0, 1)
         pack(ERR, 0, 3, on_vector)
-        multiply_both(OUT, 0, 1, [0, 1])
+        finish(ERR, 0, 2)
+        pack(ERR, 1, 2, on_scalar)
+        multiply_both(OUT, 0, 0, [0, 1])
         finish(ERR, 0, 3)
+        scale_carry(0)
         combine(ERR, 1, 0)
+        multiply_both(OUT, 0, 1, [0, 1])
         multiply_both(OUT, 0, 0, [2, 3])
         multiply_both(OUT, 0, 1, [2, 3])
+        combine(ERR, 1, 1)
         empty(OUT, 0, 0, 0)
         empty(OUT, 0, 0, 1)
-        combine(ERR, 1, 1)
         turn(ERR, 1, 3)
         empty(OUT, 0, 1, 0)
-        empty(OUT, 0, 1, 1)
-        pack(ERR, 1, 0, on_vector)
         multiply(OUT, 0, 2, 0, range(ROW_GROUPS))
         multiply(OUT, 0, 2, 1, range(ROW_GROUPS))
-        finish(ERR, 1, 2)
-        finish(ERR, 1, 0)
-        scale_carry(1)
-        combine(ERR, 1, 3)
+        pack(ERR, 1, 0, on_vector)
         pack(ERR, 1, 1, on_vector)
+        combine(ERR, 1, 3)
+        empty(OUT, 0, 1, 1)
+        finish(ERR, 1, 0)
+        finish(ERR, 1, 1)
         pack(ERR, 1, 3, on_vector)
+        scale_carry(1)
         turn(OUT, 0, 0)
         turn(OUT, 0, 1)
+        finish(ERR, 1, 2)
+        finish(ERR, 1, 3)
+        combine(OUT, 0, 0)
         empty(OUT, 0, 2, 0)
         empty(OUT, 0, 2, 1)
-        finish(ERR, 1, 1)
-        finish(ERR, 1, 3)
+        combine(OUT, 0, 1)
+        multiply_both(OUT, 1, 0, range(ROW_GROUPS))
         turn(OUT, 0, 2)
         scale_carry(2)
-        combine(OUT, 0, 0)
-        multiply_both(OUT, 1, 0, range(ROW_GROUPS))
-        store_y(0, half(0))
-        combine(OUT, 0, 1)
-        store_y(1, half(0))
-        combine(OUT, 0, 2)
-        store_y(2, half(0))
-        multiply(OUT, 1, 1, 0, range(ROW_GROUPS))
+        store_y(0, 0)
+        store_y(1, 0)
+        pack(OUT, 0, 0, on_vector)
         empty(OUT, 1, 0, 0)
         empty(OUT, 1, 0, 1)
-        turn(OUT, 1, 0)
-        pack(OUT, 0, 0, on_vector)
-        empty(OUT, 1, 1, 0)
+        multiply(OUT, 1, 1, 0, range(ROW_GROUPS))
         multiply(OUT, 1, 1, 1, range(ROW_GROUPS))
-        pack(OUT, 0, 1, on_scalar)
-        combine(OUT, 1, 0)
-        multiply(OUT, 1, 2, 0, range(ROW_GROUPS))
-        pack(OUT, 0, 2, on_vector)
-        empty(OUT, 1, 1, 1)
-        store_y(0, half(1))
+        combine(OUT, 0, 2)
+        store_y(2, 0)
+        pack(OUT, 0, 1, on_vector)
         finish(OUT, 0, 0)
+        store_codes(0, 0, nc.sync)
+        empty(OUT, 1, 1, 0)
+        empty(OUT, 1, 1, 1)
+        turn(OUT, 1, 0)
         turn(OUT, 1, 1)
+        combine(OUT, 1, 0)
+        store_y(0, 1)
+        pack(OUT, 0, 2, on_scalar)
+        multiply(OUT, 1, 2, 0, range(ROW_GROUPS))
+        multiply(OUT, 1, 2, 1, range(ROW_GROUPS))
+        combine(OUT, 1, 1)
+        store_y(1, 1)
         finish(OUT, 0, 1)
         empty(OUT, 1, 2, 0)
-        finish(OUT, 0, 2)
-        store_codes(0, 0, nc.sync)
-        store_codes(1, 0, nc.sync)
-        store_codes(2, 0, nc.sync)
-        pack(OUT, 1, 0, on_scalar)
-        combine(OUT, 1, 1)
-        last_turn(0)
-        multiply(OUT, 1, 2, 1, range(ROW_GROUPS))
-        last_combine(0)
-        store_y(1, half(1))
         pack(OUT, 1, 1, on_vector)
         empty(OUT, 1, 2, 1)
-        store_y(LAST, targets(1, 0))
-        last_pack(0, on_scalar)
-        finish(OUT, 1, 0)
+        finish(OUT, 0, 2)
+        store_codes(1, 0, nc.sync)
+        store_codes(2, 0, nc.sync)
+        last_turn(0)
         last_turn(1)
+        last_combine(0)
+        last_store(0)
+        pack(OUT, 1, 0, on_scalar)
         finish(OUT, 1, 1)
-        store_codes(0, 1, nc.sync)
         store_codes(1, 1, nc.sync)
         last_combine(1)
+        last_store(1)
+        last_pack(0, on_scalar)
         last_pack(1, on_vector)
-        store_y(LAST, targets(1, 1))
+        finish(OUT, 1, 0)
+        store_codes(0, 1, nc.sync)
         last_finish(0)
         last_finish(1)
         store_codes(2, 1, nc.scalar)

@@ -26,6 +26,9 @@ WORD4 = 2
 QUADRANT = 32
 SCALE_RUN = 4
 BANKS = 8
+RUN = 4
+STAGING_TILES = 12
+PIECE_TILES = 4
 EARLY_ROWS = 2 * GROUP
 DIRECT = 2
 LAST = FEATURE_GROUPS - 1
@@ -63,7 +66,9 @@ def tile_preconditioned_logistic_gradient_h1_kernel(
             return slice(HALF * h + P * i, HALF * h + P * (i + 1))
 
         a_early = kept("a_early", [P, FEATURE_GROUPS, WORD4 * EARLY_ROWS], U8)
-        a_late = {g: kept("a_late%d" % g, [P, FEATURE_GROUPS, WORD4 * GROUP], U8) for g in range(2, ROW_GROUPS)}
+        a_late = {
+            g: kept("a_late%d" % g, [P, FEATURE_GROUPS, WORD4 * GROUP], U8) for g in range(EARLY_ROWS // GROUP, ROW_GROUPS)
+        }
         a_sc = [kept("a_sc%d" % n, [P, FEATURE_GROUPS, EARLY_ROWS], U8) for n in range(2)]
         f_sb = [kept("f_sb%d" % n, [P, ROW_GROUPS, WORD4 * GROUP], U8) for n in range(FEATURE_GROUPS)]
         f_sc = kept("f_sc", [P, ROW_GROUPS, D], U8)
@@ -85,7 +90,6 @@ def tile_preconditioned_logistic_gradient_h1_kernel(
         direct_e = kept("direct_e", [P, SLOTS, C], BF16)
         last_packed = kept("last_packed", [P, HALF, SLOTS], BF16)
         w_bf = kept("w_bf", [P, ROW_GROUPS, SLOTS], BF16)
-        w_f32 = kept("w_f32", [P, ROW_GROUPS, SLOTS], F32)
         d_bf = kept("d_bf", [P, FEATURE_GROUPS, SLOTS], BF16)
         d_f32 = kept("d_f32", [P, FEATURE_GROUPS, SLOTS], F32)
         ident = kept("ident", [P, P], F32)
@@ -124,11 +128,9 @@ def tile_preconditioned_logistic_gradient_h1_kernel(
         def load_factors():
             nc.sync.dma_start(out=w_bf[:], in_=row_weight.rearrange("(g p t) -> p g t", p=P, t=SLOTS))
             nc.sync.dma_start(out=d_bf[:], in_=diag.rearrange("(g p t) -> p g t", p=P, t=SLOTS))
-            nc.gpsimd.tensor_copy(out=w_f32[:], in_=w_bf[:])
-            nc.gpsimd.tensor_copy(out=d_f32[:], in_=d_bf[:])
 
         def side_by_side(copy, dst, src):
-            copy(out=dst.rearrange("p (c i) t -> p c t i", i=4), in_=src.rearrange("p t (c i) -> p c t i", i=4))
+            copy(out=dst.rearrange("p (c i) t -> p c t i", i=RUN), in_=src.rearrange("p t (c i) -> p c t i", i=RUN))
 
         def quantize(codes, scales, src):
             nc.vector.quantize_mx(out=codes.bitcast(FP8X4), scales=scales, in_=src.rearrange("p c t -> p (c t)"))
@@ -142,8 +144,11 @@ def tile_preconditioned_logistic_gradient_h1_kernel(
         def weigh_labels(g):
             for t in range(SLOTS):
                 nc.vector.tensor_scalar(
-                    out=lw_sb[g][:, t, :], in0=lab_sb[g][:, t, :], scalar1=w_f32[:, g, t : t + 1], scalar2=None, op0=ALU.mult
+                    out=lw_sb[g][:, t, :], in0=lab_sb[g][:, t, :], scalar1=w_bf[:, g, t : t + 1], scalar2=None, op0=ALU.mult
                 )
+
+        def widen_diag():
+            nc.scalar.copy(out=d_f32[:], in_=d_bf[:])
 
         def scale_carry(g):
             for t in range(SLOTS):
@@ -157,7 +162,7 @@ def tile_preconditioned_logistic_gradient_h1_kernel(
 
         def errors_slot(dst, prob, g, t, cols):
             nc.vector.scalar_tensor_tensor(
-                out=dst, in0=prob, scalar=w_f32[:, g, t : t + 1], in1=lw_sb[g][:, t, cols], op0=ALU.mult, op1=ALU.subtract
+                out=dst, in0=prob, scalar=w_bf[:, g, t : t + 1], in1=lw_sb[g][:, t, cols], op0=ALU.mult, op1=ALU.subtract
             )
 
         def outputs_slot(y, grad, g, t):
@@ -193,7 +198,7 @@ def tile_preconditioned_logistic_gradient_h1_kernel(
                 multiply(kind, h, g, 1, [k])
 
         def staging():
-            return work.tile([P, SLOTS, P], F32, name="staging", bufs=12)
+            return work.tile([P, SLOTS, P], F32, name="staging", bufs=STAGING_TILES)
 
         def empty(kind, h, g, i):
             key = (kind, h, g, i)
@@ -216,7 +221,7 @@ def tile_preconditioned_logistic_gradient_h1_kernel(
         def combine(kind, h, g):
             pair = turned[(kind, h, g)]
             if kind == ERR:
-                e_by_slot = work.tile([P, SLOTS, HALF], BF16, name="e_by_slot", bufs=4)
+                e_by_slot = work.tile([P, SLOTS, HALF], BF16, name="e_by_slot", bufs=PIECE_TILES)
                 by_slot[(kind, h, g)] = e_by_slot[:]
             else:
                 by_slot[(kind, h, g)] = y_sb[g][:, :, half(h)]
@@ -230,7 +235,7 @@ def tile_preconditioned_logistic_gradient_h1_kernel(
                     give_bank((kind, h, g, "turned", t // 2))
 
         def pack(kind, h, g, copy):
-            packed[(kind, h, g)] = work.tile([P, HALF, SLOTS], BF16, name="packed", bufs=4, align_bytes=64)
+            packed[(kind, h, g)] = work.tile([P, HALF, SLOTS], BF16, name="packed", bufs=PIECE_TILES, align_bytes=64)
             side_by_side(copy, packed[(kind, h, g)][:], by_slot[(kind, h, g)])
 
         def finish(kind, h, g):
@@ -312,11 +317,12 @@ def tile_preconditioned_logistic_gradient_h1_kernel(
                 in_=y_q[g][:, half(h)].bitcast(I32),
             )
 
-        for plane in a_sc:
-            nc.vector.memset(plane[:].bitcast(I32), 0)
+        nc.vector.memset(a_sc[0][:].bitcast(I32), 0)
         nc.vector.memset(warm[:], 0.0)
-        make_identity(nc, ident[:])
-        nc.gpsimd.memset(f_sc[:].bitcast(I32), 0)
+        nc.vector.memset(ident[:], 0.0)
+        make_identity(nc, ident[:], nomemset=True)
+        nc.vector.memset(a_sc[1][:].bitcast(I32), 0)
+        nc.vector.memset(f_sc[:].bitcast(I32), 0)
         nc.scalar.activation(out=warm[:], in_=warm[:], func=ACT.Sigmoid)
 
         load_rows(coef_sb, coef, 0)
@@ -342,26 +348,25 @@ def tile_preconditioned_logistic_gradient_h1_kernel(
         load_f(2)
         load_rows(carry_sb, carry, 2)
 
+
         coef_pack(0, half(0), on_vector)
-        coef_pack(0, targets(1, 0), on_scalar)
+        coef_pack(0, half(1), on_scalar)
         coef_quantize(0, half(0))
         multiply_both(ERR, 0, 0, [0])
         multiply_both(ERR, 0, 1, [0])
-        coef_pack(0, targets(1, 1), on_vector)
         coef_quantize(0, half(1))
         multiply_both(ERR, 1, 0, [0])
         multiply_both(ERR, 1, 1, [0])
         coef_pack(1, half(0), on_vector)
         coef_pack(1, half(1), on_scalar)
-        coef_pack(2, half(0), on_vector)
         coef_quantize(1, half(0))
-        coef_quantize(1, half(1))
+        coef_pack(2, half(0), on_vector)
         coef_pack(2, half(1), on_scalar)
         coef_quantize(2, half(0))
+        coef_quantize(1, half(1))
         multiply_both(ERR, 0, 0, [1])
         multiply_both(ERR, 0, 1, [1])
         multiply_both(ERR, 1, 0, [1])
-        reorder_words(0)
         coef_quantize(2, half(1))
         multiply_both(ERR, 0, 0, [2])
         empty(ERR, 0, 0, 0)
@@ -370,11 +375,14 @@ def tile_preconditioned_logistic_gradient_h1_kernel(
         multiply_both(ERR, 1, 1, [1])
         multiply_both(ERR, 1, 0, [2])
         multiply_both(ERR, 1, 1, [2])
-        reorder_scales()
+
+        reorder_words(0)
         reorder_words(1)
         reorder_words(2)
+        reorder_scales()
         empty(ERR, 0, 1, 0)
         empty(ERR, 0, 1, 1)
+
         turn(ERR, 0, 0)
         turn(ERR, 0, 1)
         empty(ERR, 1, 0, 0)
@@ -382,17 +390,19 @@ def tile_preconditioned_logistic_gradient_h1_kernel(
         empty(ERR, 1, 1, 0)
         empty(ERR, 1, 1, 1)
         weigh_labels(0)
+        weigh_labels(1)
         combine(ERR, 0, 0)
         direct_multiply(0)
         direct_multiply(1)
-        weigh_labels(1)
         direct_empty(0)
+        weigh_labels(2)
         combine(ERR, 0, 1)
         direct_multiply(2)
         direct_multiply(3)
+        widen_diag()
         pack(ERR, 0, 0, on_scalar)
-        weigh_labels(2)
         direct_empty(1)
+        weigh_labels(3)
         direct_combine(0)
         finish(ERR, 0, 0)
         multiply(ERR, 0, 3, 0, range(FEATURE_GROUPS))
@@ -400,25 +410,25 @@ def tile_preconditioned_logistic_gradient_h1_kernel(
         direct_empty(2)
         direct_empty(3)
         direct_combine(1)
-        weigh_labels(3)
         direct_combine(2)
         direct_combine(3)
         multiply(ERR, 1, 3, 0, range(FEATURE_GROUPS))
         multiply(ERR, 1, 3, 1, range(FEATURE_GROUPS))
         empty(ERR, 0, 3, 0)
         empty(ERR, 0, 3, 1)
+
         turn(ERR, 0, 3)
+        pack(ERR, 0, 1, on_scalar)
         empty(ERR, 1, 3, 0)
         empty(ERR, 1, 3, 1)
         turn(ERR, 1, 0)
         turn(ERR, 1, 1)
-        pack(ERR, 0, 1, on_vector)
         pack(ERR, 0, 2, on_scalar)
-        combine(ERR, 0, 3)
         finish(ERR, 0, 1)
+        combine(ERR, 0, 3)
         pack(ERR, 0, 3, on_vector)
         finish(ERR, 0, 2)
-        pack(ERR, 1, 2, on_scalar)
+
         multiply_both(OUT, 0, 0, [0, 1])
         finish(ERR, 0, 3)
         scale_carry(0)
@@ -433,14 +443,16 @@ def tile_preconditioned_logistic_gradient_h1_kernel(
         empty(OUT, 0, 1, 0)
         multiply(OUT, 0, 2, 0, range(ROW_GROUPS))
         multiply(OUT, 0, 2, 1, range(ROW_GROUPS))
+        pack(ERR, 1, 2, on_vector)
         pack(ERR, 1, 0, on_vector)
-        pack(ERR, 1, 1, on_vector)
+        pack(ERR, 1, 1, on_scalar)
         combine(ERR, 1, 3)
         empty(OUT, 0, 1, 1)
         finish(ERR, 1, 0)
         finish(ERR, 1, 1)
         pack(ERR, 1, 3, on_vector)
         scale_carry(1)
+
         turn(OUT, 0, 0)
         turn(OUT, 0, 1)
         finish(ERR, 1, 2)
@@ -464,8 +476,11 @@ def tile_preconditioned_logistic_gradient_h1_kernel(
         pack(OUT, 0, 1, on_vector)
         finish(OUT, 0, 0)
         store_codes(0, 0, nc.sync)
+        finish(OUT, 0, 1)
+        store_codes(1, 0, nc.sync)
         empty(OUT, 1, 1, 0)
         empty(OUT, 1, 1, 1)
+
         turn(OUT, 1, 0)
         turn(OUT, 1, 1)
         combine(OUT, 1, 0)
@@ -475,12 +490,10 @@ def tile_preconditioned_logistic_gradient_h1_kernel(
         multiply(OUT, 1, 2, 1, range(ROW_GROUPS))
         combine(OUT, 1, 1)
         store_y(1, 1)
-        finish(OUT, 0, 1)
         empty(OUT, 1, 2, 0)
         pack(OUT, 1, 1, on_vector)
         empty(OUT, 1, 2, 1)
         finish(OUT, 0, 2)
-        store_codes(1, 0, nc.sync)
         store_codes(2, 0, nc.sync)
         last_turn(0)
         last_turn(1)
@@ -492,8 +505,8 @@ def tile_preconditioned_logistic_gradient_h1_kernel(
         last_combine(1)
         last_store(1)
         last_pack(0, on_scalar)
-        last_pack(1, on_vector)
         finish(OUT, 1, 0)
+        last_pack(1, on_vector)
         store_codes(0, 1, nc.sync)
         last_finish(0)
         last_finish(1)

from contextlib import ExitStack

import concourse.mybir as mybir
from concourse.masks import make_identity

R, D, C = 2048, 1536, 512
FLOPS = 2 * 2 * R * D * C

F32 = mybir.dt.float32
BF16 = mybir.dt.bfloat16
I32 = mybir.dt.int32
U32 = mybir.dt.uint32
U8 = mybir.dt.uint8
FP8X4 = mybir.dt.float8_e4m3fn_x4
FP4X4 = mybir.dt.float4_e2m1fn_x4
ALU = mybir.AluOpType
ACT = mybir.ActivationFunctionType

P = 128
SLOTS = 4
GROUP = P * SLOTS
FEATURE_GROUPS = D // GROUP
ROW_GROUPS = R // GROUP
HALF = C // 2
WORD4 = 2
QUADRANT = 32
SCALE_RUN = 4
BANKS = 8
RUN = 4
STAGING_TILES = 12
PIECE_TILES = 4
EARLY_ROWS = 2 * GROUP
DIRECT = 2
LAST = FEATURE_GROUPS - 1
ERR, OUT = "errors", "outputs"


def tile_preconditioned_logistic_gradient_h1_kernel(
    tc, a_words, a_scales, f_words, f_scales, coef, labels, row_weight, carry, diag, out_0, out_1, out_2
):
    nc = tc.nc
    with ExitStack() as ctx:
        keep = ctx.enter_context(tc.tile_pool(name="keep", bufs=1))
        work = ctx.enter_context(tc.tile_pool(name="work", bufs=1))
        psum = ctx.enter_context(tc.psum_pool(name="psum", bufs=1))
        ctx.enter_context(tc.manual_schedule())
        on_vector, on_scalar = nc.vector.tensor_copy, nc.scalar.copy

        def kept(name, shape, dtype):
            return keep.tile(shape, dtype, name=name, align_bytes=64)

        free_banks = list(range(BANKS))
        bank_of = {}

        def take_bank(key):
            bank_of[key] = free_banks.pop(0)
            return psum.tile([P, GROUP], F32, name="bank%d" % bank_of[key])

        def give_bank(key):
            free_banks.append(bank_of[key])

        def half(h):
            return slice(HALF * h, HALF * (h + 1))

        def targets(h, i):
            return slice(HALF * h + P * i, HALF * h + P * (i + 1))

        a_early = kept("a_early", [P, FEATURE_GROUPS, WORD4 * EARLY_ROWS], U8)
        a_late = {
            g: kept("a_late%d" % g, [P, FEATURE_GROUPS, WORD4 * GROUP], U8) for g in range(EARLY_ROWS // GROUP, ROW_GROUPS)
        }
        a_sc = [kept("a_sc%d" % n, [P, FEATURE_GROUPS, EARLY_ROWS], U8) for n in range(2)]
        f_sb = [kept("f_sb%d" % n, [P, ROW_GROUPS, WORD4 * GROUP], U8) for n in range(FEATURE_GROUPS)]
        f_sc = kept("f_sc", [P, ROW_GROUPS, D], U8)
        coef_sb = [kept("coef_sb%d" % n, [P, SLOTS, C], BF16) for n in range(FEATURE_GROUPS)]
        coef_packed = [kept("coef_packed%d" % n, [P, C, SLOTS], BF16) for n in range(FEATURE_GROUPS)]
        coef_q = [kept("coef_q%d" % n, [P, C], U32) for n in range(FEATURE_GROUPS)]
        coef_s = [kept("coef_s%d" % n, [P, C], U8) for n in range(FEATURE_GROUPS)]
        lab_sb = [kept("lab_sb%d" % n, [P, SLOTS, C], BF16) for n in range(ROW_GROUPS)]
        lw_sb = [kept("lw_sb%d" % n, [P, SLOTS, C], BF16) for n in range(ROW_GROUPS)]
        e_q = [kept("e_q%d" % n, [P, C], U32) for n in range(ROW_GROUPS)]
        e_s = [kept("e_s%d" % n, [P, C], U8) for n in range(ROW_GROUPS)]
        carry_sb = [kept("carry_sb%d" % n, [P, SLOTS, C], BF16) for n in range(FEATURE_GROUPS)]
        y_sb = [kept("y_sb%d" % n, [P, SLOTS, HALF if n == LAST else C], F32) for n in range(FEATURE_GROUPS)]
        y_last = kept("y_last", [P, 2, SLOTS, P], F32)
        y_q = [kept("y_q%d" % n, [P, C], U32) for n in range(FEATURE_GROUPS)]
        y_s = kept("y_s", [P, FEATURE_GROUPS, C], U8)
        direct_sb = kept("direct_sb", [P, FEATURE_GROUPS, WORD4 * GROUP], U8)
        direct_sc = kept("direct_sc", [P, FEATURE_GROUPS, GROUP], U8)
        direct_e = kept("direct_e", [P, SLOTS, C], BF16)
        last_packed = kept("last_packed", [P, HALF, SLOTS], BF16)
        w_bf = kept("w_bf", [P, ROW_GROUPS, SLOTS], BF16)
        d_bf = kept("d_bf", [P, FEATURE_GROUPS, SLOTS], BF16)
        d_f32 = kept("d_f32", [P, FEATURE_GROUPS, SLOTS], F32)
        ident = kept("ident", [P, P], F32)
        warm = kept("warm", [P, 1], F32)

        sums = {}
        emptied = {}
        turned = {}
        by_slot = {}
        packed = {}

        a_by_p = a_words.rearrange("g p n -> p g n")
        f_by_p = f_words.rearrange("g p n -> p g n")

        def load_rows(dst, src, g):
            nc.sync.dma_start(out=dst[g][:], in_=src[g * GROUP : (g + 1) * GROUP, :].rearrange("(p t) c -> p t c", t=SLOTS))

        def load_scale_rows(plane, rows):
            by_r = rows.rearrange("g (q r) n -> r q g n", r=SCALE_RUN)
            for r in range(SCALE_RUN):
                nc.sync.dma_start(out=plane[r:P:QUADRANT, :, :].bitcast(I32), in_=by_r[r].bitcast(I32))

        def load_a_early(k):
            nc.sync.dma_start(out=a_early[:, k, :].bitcast(I32), in_=a_by_p[:, k, 0 : WORD4 * EARLY_ROWS].bitcast(I32))

        def load_a_late(g):
            nc.sync.dma_start(
                out=a_late[g][:].bitcast(I32), in_=a_by_p[:, :, WORD4 * GROUP * g : WORD4 * GROUP * (g + 1)].bitcast(I32)
            )

        def load_f(g):
            nc.sync.dma_start(
                out=f_sb[g][:].bitcast(I32), in_=f_by_p[:, :, WORD4 * GROUP * g : WORD4 * GROUP * (g + 1)].bitcast(I32)
            )

        def load_factors():
            nc.sync.dma_start(out=w_bf[:], in_=row_weight.rearrange("(g p t) -> p g t", p=P, t=SLOTS))
            nc.sync.dma_start(out=d_bf[:], in_=diag.rearrange("(g p t) -> p g t", p=P, t=SLOTS))

        def side_by_side(copy, dst, src):
            copy(out=dst.rearrange("p (c i) t -> p c t i", i=RUN), in_=src.rearrange("p t (c i) -> p c t i", i=RUN))

        def quantize(codes, scales, src):
            nc.vector.quantize_mx(out=codes.bitcast(FP8X4), scales=scales, in_=src.rearrange("p c t -> p (c t)"))

        def coef_pack(k, cols, copy):
            side_by_side(copy, coef_packed[k][:, cols, :], coef_sb[k][:, :, cols])

        def coef_quantize(k, cols):
            quantize(coef_q[k][:, cols], coef_s[k][:, cols], coef_packed[k][:, cols, :])

        def weigh_labels(g):
            for t in range(SLOTS):
                nc.vector.tensor_scalar(
                    out=lw_sb[g][:, t, :], in0=lab_sb[g][:, t, :], scalar1=w_bf[:, g, t : t + 1], scalar2=None, op0=ALU.mult
                )

        def widen_diag():
            nc.scalar.copy(out=d_f32[:], in_=d_bf[:])

        def scale_carry(g):
            for t in range(SLOTS):
                if g == LAST:
                    last_carry = carry_sb[g][:, t, half(1)].rearrange("p (i c) -> p i c", i=2)
                    parts = [(y_sb[g][:, t, :], carry_sb[g][:, t, half(0)]), (y_last[:, :, t, :], last_carry)]
                else:
                    parts = [(y_sb[g][:, t, :], carry_sb[g][:, t, :])]
                for dst, src in parts:
                    nc.scalar.activation(out=dst, in_=src, func=ACT.Copy, scale=d_f32[:, g, t : t + 1])

        def errors_slot(dst, prob, g, t, cols):
            nc.vector.scalar_tensor_tensor(
                out=dst, in0=prob, scalar=w_bf[:, g, t : t + 1], in1=lw_sb[g][:, t, cols], op0=ALU.mult, op1=ALU.subtract
            )

        def outputs_slot(y, grad, g, t):
            nc.vector.scalar_tensor_tensor(out=y, in0=grad, scalar=d_f32[:, g, t : t + 1], in1=y, op0=ALU.mult, op1=ALU.add)

        def multiply(kind, h, g, i, passes):
            key = (kind, h, g, i)
            cols = targets(h, i)
            for k in passes:
                if k == 0:
                    sums[key] = take_bank(key)
                if kind == ERR:
                    n, lo = divmod(GROUP * g, EARLY_ROWS)
                    codes, scales, count = coef_q[k], coef_s[k], FEATURE_GROUPS
                    words = a_late[g][:, k, :] if n else a_early[:, k, WORD4 * lo : WORD4 * (lo + GROUP)]
                    word_scales = a_sc[n][:, k, lo : lo + GROUP]
                else:
                    codes, scales, count = e_q[k], e_s[k], ROW_GROUPS
                    words, word_scales = f_sb[g][:, k, :], f_sc[:, k, GROUP * g : GROUP * (g + 1)]
                nc.tensor.matmul_mx(
                    out=sums[key][:],
                    lhsT=codes[:, cols].bitcast(FP8X4),
                    lhsT_scale=scales[:, cols],
                    rhs=words.bitcast(FP4X4),
                    rhs_scale=word_scales,
                    start=(k == 0),
                    stop=(k == count - 1),
                )

        def multiply_both(kind, h, g, passes):
            for k in passes:
                multiply(kind, h, g, 0, [k])
                multiply(kind, h, g, 1, [k])

        def staging():
            return work.tile([P, SLOTS, P], F32, name="staging", bufs=STAGING_TILES)

        def empty(kind, h, g, i):
            key = (kind, h, g, i)
            src = sums[key][:].rearrange("c (p t) -> c t p", t=SLOTS)
            emptied[key] = staging()
            if kind == ERR:
                nc.scalar.activation(out=emptied[key][:], in_=src, func=ACT.Sigmoid)
            else:
                nc.scalar.copy(out=emptied[key][:], in_=src)
            give_bank(key)

        def turn(kind, h, g):
            pair = [take_bank((kind, h, g, "turned", u)) for u in range(2)]
            turned[(kind, h, g)] = pair
            for i in range(2):
                for t in range(SLOTS):
                    lo = HALF * (t % 2) + P * i
                    nc.tensor.transpose(pair[t // 2][:, lo : lo + P], emptied[(kind, h, g, i)][:, t, :], ident[:])

        def combine(kind, h, g):
            pair = turned[(kind, h, g)]
            if kind == ERR:
                e_by_slot = work.tile([P, SLOTS, HALF], BF16, name="e_by_slot", bufs=PIECE_TILES)
                by_slot[(kind, h, g)] = e_by_slot[:]
            else:
                by_slot[(kind, h, g)] = y_sb[g][:, :, half(h)]
            for t in range(SLOTS):
                src = pair[t // 2][:, HALF * (t % 2) : HALF * (t % 2 + 1)]
                if kind == ERR:
                    errors_slot(by_slot[(kind, h, g)][:, t, :], src, g, t, half(h))
                else:
                    outputs_slot(by_slot[(kind, h, g)][:, t, :], src, g, t)
                if t % 2:
                    give_bank((kind, h, g, "turned", t // 2))

        def pack(kind, h, g, copy):
            packed[(kind, h, g)] = work.tile([P, HALF, SLOTS], BF16, name="packed", bufs=PIECE_TILES, align_bytes=64)
            side_by_side(copy, packed[(kind, h, g)][:], by_slot[(kind, h, g)])

        def finish(kind, h, g):
            if kind == ERR:
                quantize(e_q[g][:, half(h)], e_s[g][:, half(h)], packed[(kind, h, g)][:])
            else:
                quantize(y_q[g][:, half(h)], y_s[:, g, half(h)], packed[(kind, h, g)][:])

        direct_lo = GROUP * DIRECT - EARLY_ROWS

        def reorder_words(k):
            nc.vector.tensor_copy(
                out=direct_sb[:, k, :].rearrange("p (t m b) -> p t m b", t=SLOTS, b=WORD4),
                in_=a_late[DIRECT][:, k, :].rearrange("p (m t b) -> p t m b", t=SLOTS, b=WORD4),
            )

        def reorder_scales():
            nc.vector.tensor_copy(
                out=direct_sc[:].rearrange("p g (t m) -> p g t m", t=SLOTS),
                in_=a_sc[1][:, :, direct_lo : direct_lo + GROUP].rearrange("p g (m t) -> p g t m", t=SLOTS),
            )

        def direct_multiply(t):
            sums[("direct", t)] = take_bank(("direct", t))
            for k in range(FEATURE_GROUPS):
                nc.tensor.matmul_mx(
                    out=sums[("direct", t)][:],
                    lhsT=direct_sb[:, k, WORD4 * P * t : WORD4 * P * (t + 1)].bitcast(FP4X4),
                    lhsT_scale=direct_sc[:, k, P * t : P * (t + 1)],
                    rhs=coef_q[k][:].bitcast(FP8X4),
                    rhs_scale=coef_s[k][:],
                    start=(k == 0),
                    stop=(k == FEATURE_GROUPS - 1),
                )

        def direct_empty(t):
            emptied[("direct", t)] = staging()
            nc.scalar.activation(
                out=emptied[("direct", t)][:].rearrange("p a b -> p (a b)"), in_=sums[("direct", t)][:], func=ACT.Sigmoid
            )
            give_bank(("direct", t))

        def direct_combine(t):
            errors_slot(direct_e[:, t, :], emptied[("direct", t)][:].rearrange("p a b -> p (a b)"), DIRECT, t, slice(0, C))

        for h in range(2):
            by_slot[(ERR, h, DIRECT)] = direct_e[:, :, half(h)]

        def last_turn(i):
            turned[("last", i)] = take_bank(("last", i))
            for t in range(SLOTS):
                nc.tensor.transpose(
                    turned[("last", i)][:, P * t : P * (t + 1)], emptied[(OUT, 1, LAST, i)][:, t, :], ident[:]
                )

        def last_combine(i):
            for t in range(SLOTS):
                outputs_slot(y_last[:, i, t, :], turned[("last", i)][:, P * t : P * (t + 1)], LAST, t)
            give_bank(("last", i))

        def last_pack(i, copy):
            side_by_side(copy, last_packed[:, targets(0, i), :], y_last[:, i, :, :])

        def last_finish(i):
            quantize(y_q[LAST][:, targets(1, i)], y_s[:, LAST, targets(1, i)], last_packed[:, targets(0, i), :])

        def store_rows(g, cols, src):
            nc.sync.dma_start(out=out_0[g * GROUP : (g + 1) * GROUP, cols].rearrange("(p t) c -> p t c", t=SLOTS), in_=src)

        def store_y(g, h):
            store_rows(g, half(h), y_sb[g][:, :, half(h)])

        def last_store(i):
            store_rows(LAST, targets(1, i), y_last[:, i, :, :])

        def store_codes(g, h, queue):
            queue.dma_start(
                out=out_1[g].rearrange("p c t -> p (c t)")[:, SLOTS * HALF * h : SLOTS * HALF * (h + 1)].bitcast(I32),
                in_=y_q[g][:, half(h)].bitcast(I32),
            )

        nc.vector.memset(a_sc[0][:].bitcast(I32), 0)
        nc.vector.memset(warm[:], 0.0)
        nc.vector.memset(ident[:], 0.0)
        make_identity(nc, ident[:], nomemset=True)
        nc.vector.memset(a_sc[1][:].bitcast(I32), 0)
        nc.vector.memset(f_sc[:].bitcast(I32), 0)
        nc.scalar.activation(out=warm[:], in_=warm[:], func=ACT.Sigmoid)

        load_rows(coef_sb, coef, 0)
        load_scale_rows(a_sc[0], a_scales[:, :, 0:EARLY_ROWS])
        load_a_early(0)
        load_rows(coef_sb, coef, 1)
        load_rows(coef_sb, coef, 2)
        load_a_early(1)
        load_a_late(2)
        load_a_early(2)
        load_scale_rows(a_sc[1], a_scales[:, :, EARLY_ROWS:])
        load_factors()
        load_rows(lab_sb, labels, 0)
        load_a_late(3)
        load_rows(lab_sb, labels, 1)
        load_rows(lab_sb, labels, 2)
        load_rows(lab_sb, labels, 3)
        load_scale_rows(f_sc, f_scales)
        load_f(0)
        load_rows(carry_sb, carry, 0)
        load_f(1)
        load_rows(carry_sb, carry, 1)
        load_f(2)
        load_rows(carry_sb, carry, 2)


        coef_pack(0, half(0), on_vector)
        coef_pack(0, half(1), on_scalar)
        coef_quantize(0, half(0))
        multiply_both(ERR, 0, 0, [0])
        multiply_both(ERR, 0, 1, [0])
        coef_quantize(0, half(1))
        multiply_both(ERR, 1, 0, [0])
        multiply_both(ERR, 1, 1, [0])
        coef_pack(1, half(0), on_vector)
        coef_pack(1, half(1), on_scalar)
        coef_quantize(1, half(0))
        coef_pack(2, half(0), on_vector)
        coef_pack(2, half(1), on_scalar)
        coef_quantize(2, half(0))
        coef_quantize(1, half(1))
        multiply_both(ERR, 0, 0, [1])
        multiply_both(ERR, 0, 1, [1])
        multiply_both(ERR, 1, 0, [1])
        coef_quantize(2, half(1))
        multiply_both(ERR, 0, 0, [2])
        empty(ERR, 0, 0, 0)
        empty(ERR, 0, 0, 1)
        multiply_both(ERR, 0, 1, [2])
        multiply_both(ERR, 1, 1, [1])
        multiply_both(ERR, 1, 0, [2])
        multiply_both(ERR, 1, 1, [2])

        reorder_words(0)
        reorder_words(1)
        reorder_words(2)
        reorder_scales()
        empty(ERR, 0, 1, 0)
        empty(ERR, 0, 1, 1)

        turn(ERR, 0, 0)
        turn(ERR, 0, 1)
        empty(ERR, 1, 0, 0)
        empty(ERR, 1, 0, 1)
        empty(ERR, 1, 1, 0)
        empty(ERR, 1, 1, 1)
        weigh_labels(0)
        weigh_labels(1)
        combine(ERR, 0, 0)
        direct_multiply(0)
        direct_multiply(1)
        direct_empty(0)
        weigh_labels(2)
        combine(ERR, 0, 1)
        direct_multiply(2)
        direct_multiply(3)
        widen_diag()
        pack(ERR, 0, 0, on_scalar)
        direct_empty(1)
        weigh_labels(3)
        direct_combine(0)
        finish(ERR, 0, 0)
        multiply(ERR, 0, 3, 0, range(FEATURE_GROUPS))
        multiply(ERR, 0, 3, 1, range(FEATURE_GROUPS))
        direct_empty(2)
        direct_empty(3)
        direct_combine(1)
        direct_combine(2)
        direct_combine(3)
        multiply(ERR, 1, 3, 0, range(FEATURE_GROUPS))
        multiply(ERR, 1, 3, 1, range(FEATURE_GROUPS))
        empty(ERR, 0, 3, 0)
        empty(ERR, 0, 3, 1)

        turn(ERR, 0, 3)
        pack(ERR, 0, 1, on_scalar)
        empty(ERR, 1, 3, 0)
        empty(ERR, 1, 3, 1)
        turn(ERR, 1, 0)
        turn(ERR, 1, 1)
        pack(ERR, 0, 2, on_scalar)
        finish(ERR, 0, 1)
        combine(ERR, 0, 3)
        pack(ERR, 0, 3, on_vector)
        finish(ERR, 0, 2)

        multiply_both(OUT, 0, 0, [0, 1])
        finish(ERR, 0, 3)
        scale_carry(0)
        combine(ERR, 1, 0)
        multiply_both(OUT, 0, 1, [0, 1])
        multiply_both(OUT, 0, 0, [2, 3])
        multiply_both(OUT, 0, 1, [2, 3])
        combine(ERR, 1, 1)
        empty(OUT, 0, 0, 0)
        empty(OUT, 0, 0, 1)
        turn(ERR, 1, 3)
        empty(OUT, 0, 1, 0)
        multiply(OUT, 0, 2, 0, range(ROW_GROUPS))
        multiply(OUT, 0, 2, 1, range(ROW_GROUPS))
        pack(ERR, 1, 2, on_vector)
        pack(ERR, 1, 0, on_vector)
        pack(ERR, 1, 1, on_scalar)
        combine(ERR, 1, 3)
        empty(OUT, 0, 1, 1)
        finish(ERR, 1, 0)
        finish(ERR, 1, 1)
        pack(ERR, 1, 3, on_vector)
        scale_carry(1)

        turn(OUT, 0, 0)
        turn(OUT, 0, 1)
        finish(ERR, 1, 2)
        finish(ERR, 1, 3)
        combine(OUT, 0, 0)
        empty(OUT, 0, 2, 0)
        empty(OUT, 0, 2, 1)
        combine(OUT, 0, 1)
        multiply_both(OUT, 1, 0, range(ROW_GROUPS))
        turn(OUT, 0, 2)
        scale_carry(2)
        store_y(0, 0)
        store_y(1, 0)
        pack(OUT, 0, 0, on_vector)
        empty(OUT, 1, 0, 0)
        empty(OUT, 1, 0, 1)
        multiply(OUT, 1, 1, 0, range(ROW_GROUPS))
        multiply(OUT, 1, 1, 1, range(ROW_GROUPS))
        combine(OUT, 0, 2)
        store_y(2, 0)
        pack(OUT, 0, 1, on_vector)
        finish(OUT, 0, 0)
        store_codes(0, 0, nc.sync)
        finish(OUT, 0, 1)
        store_codes(1, 0, nc.sync)
        empty(OUT, 1, 1, 0)
        empty(OUT, 1, 1, 1)

        turn(OUT, 1, 0)
        turn(OUT, 1, 1)
        combine(OUT, 1, 0)
        store_y(0, 1)
        pack(OUT, 0, 2, on_scalar)
        multiply(OUT, 1, 2, 0, range(ROW_GROUPS))
        multiply(OUT, 1, 2, 1, range(ROW_GROUPS))
        combine(OUT, 1, 1)
        store_y(1, 1)
        empty(OUT, 1, 2, 0)
        pack(OUT, 1, 1, on_vector)
        empty(OUT, 1, 2, 1)
        finish(OUT, 0, 2)
        store_codes(2, 0, nc.sync)
        last_turn(0)
        last_turn(1)
        last_combine(0)
        last_store(0)
        pack(OUT, 1, 0, on_scalar)
        finish(OUT, 1, 1)
        store_codes(1, 1, nc.sync)
        last_combine(1)
        last_store(1)
        last_pack(0, on_scalar)
        finish(OUT, 1, 0)
        last_pack(1, on_vector)
        store_codes(0, 1, nc.sync)
        last_finish(0)
        last_finish(1)
        store_codes(2, 1, nc.scalar)

        by_r = out_2.rearrange("g (q r) c -> r q g c", r=SCALE_RUN)
        for r in range(SCALE_RUN):
            queue = nc.scalar if r % 2 else nc.sync
            queue.dma_start(out=by_r[r].bitcast(I32), in_=y_s[r:P:QUADRANT, :, :].bitcast(I32))
